import numpy as np, ml_dtypes
CORES = [24,25,26,27,28,29,30,31]
N = 8
import mx_ref
BF = ml_dtypes.bfloat16
def gcols(t, e):
    v = np.concatenate([t.reshape(8, 16, -1, 4), np.zeros((8, 16, 1, 4), BF)], axis=2)
    return np.ascontiguousarray(np.stack([v[g][:, e[g]] for g in range(8)])).reshape(128, -1)
def tile(rs):
    return np.stack(rs, axis=2).reshape(128, -1).astype(BF)
def cut(t, i, w=512):
    return t[:, w * i:w * i + w]
def pick(q, e):
    c = np.concatenate([q[0].reshape(128, -1, 4), np.zeros((128, 1, 4), np.uint8)], axis=1); s = np.concatenate([q[1], np.ones((16, 1), np.uint8)], axis=1)
    return (np.ascontiguousarray(c[:, e].reshape(128, -1)), np.ascontiguousarray(s[:, e]))
def join(*qs):
    return (np.concatenate([q[0] for q in qs], axis=1), np.concatenate([q[1] for q in qs], axis=1))
def put(q, e, v):
    c, s = q[0].reshape(128, -1, 4).copy(), q[1].copy(); c[:, e] = v[0].reshape(128, -1, 4); s[:, e] = v[1]
    return (c.reshape(128, -1), s)
def pk(c, s):
    return (np.ascontiguousarray(c), mx_ref.live(s))
def emit(q):
    return q[0], q[1]
def packed(v, rng):
    q = [mx_ref.quantize(np.ascontiguousarray(v[r])) for r in range(N)]
    return np.stack([a for a, b in q]), np.stack([mx_ref.plane(b, rng) for a, b in q])
def values_of_codes():
    e, c = np.zeros((128, 128, 4), np.float32), np.zeros((128, 2, 4), np.uint8)
    e[np.arange(128), np.arange(128), 0] = 1
    c[:127, :, 0] = np.arange(256).reshape(2, 128).T[:127]
    return mx_ref.matmul(mx_ref.quantize(e.reshape(128, 512).astype(BF)), (c.reshape(128, 8), np.full((16, 2), 127, np.uint8))).T.reshape(-1).astype(np.float64)
CODE_VALUE, SCALE_VALUE = values_of_codes(), 2.0 ** (np.arange(256) - 127.0)
def decode(q):
    return (CODE_VALUE[q[0]].reshape(16, 8, -1, 4) * SCALE_VALUE[q[1]][:, None, :, None] + 0.0).reshape(128, -1).astype(np.float32)
def f(rng, *shape):
    return mx_ref.flush((rng.standard_normal(shape, dtype=np.float32) * np.exp2(rng.integers(-2, 3, shape[:-1] + (1,)))).astype(BF))
def wide(rng, *shape, cols=0):
    v = rng.standard_normal(shape, dtype=np.float32) * np.exp2(rng.integers(-12, 13, shape)).astype(np.float32)
    if cols: v *= np.repeat(np.exp2(rng.integers(-cols, cols + 1, shape[:-2] + (1, shape[-1] // 4))) * (rng.random(shape[:-2] + (1, shape[-1] // 4)) > 0.0625), 4, axis=-1).astype(np.float32)
    return mx_ref.flush(v.astype(BF))
C, A, R = 256, 144, 3
def slots(s, p):
    b = s[1] > s[0]
    late = np.where(b, s[1] > p[1], s[0] > p[0])
    c = np.sort(np.where(late, C * b + np.arange(C), 2 * C), axis=1)[:, :A]
    return np.where(c < 2 * C, c, -1)
def replaced(t, e, v):
    p = np.tile(np.arange(C + 1), (8, 1))
    p[np.arange(8)[:, None], e] = C + np.arange(A)
    return gcols(np.concatenate([t, v], axis=1), p[:, :C])
def big(v, k):
    v = v.astype(np.float32) * np.float32(k)
    v[np.abs(v) < np.float32(2.0 ** -16)] = 0
    return v.astype(BF)
def weights(rng, w):
    c, p = packed(w, rng)
    return {"wc": c, "ws": p}
def numbers_of(rng):
    return {"x": big(f(rng, N, 128, 12 * C), 1), "u": np.array(f(rng, N, 128, 512)), "v": np.array(f(rng, N, 128, 512))}
def kinds(rng):
    one = [(A, 0), (A - 1, 1), (A - 1, 2), (0, A), (0, A + 1), (1, 0), (0, 0), (C // 2, C - C // 2)]
    two = [(C, 0), (0, C), (A + 1, 0), (A - 1, 0), (0, A - 1), (0, 1), (C - 1, 1), (1, C - 1)]
    n = np.zeros((N, 8, 2), int)
    o = rng.permutation(N)
    for r in range(N):
        if o[r] > 0: n[r] = rng.permutation(np.array(two if o[r] == 1 else one))
    p = np.argsort(rng.random((N, 8, C)), axis=2)
    return (p >= n[:, :, :1]).astype(int) + (p >= n[:, :, :1] + n[:, :, 1:]).astype(int)
def marks(rng):
    c = kinds(rng)
    after = np.roll(c, -1, axis=0)
    m = np.full((N, 8, 3, C), 2)
    m[:, :, 0] = np.where(c == 0, 1, np.where(c == 1, rng.integers(1, 4, c.shape), rng.integers(2, 4, c.shape)))
    m[:, :, 2] = np.where(after == 1, 3, rng.integers(1, 3, c.shape))
    return m
def passing(rng):
    w = big(f(rng, N, 128, 2048), 1).reshape(N, 8, 16, 4, 8, 16, 4)
    w[:, :, 0] = 0
    w[:, :, 8:] = 0
    w[:, :, :, :, :, 0] = 0
    w[:, :, :, :, :, 8:] = 0
    w = w.reshape(N, 128, 4, 128, 4)
    for i in range(0, 128, 8):
        for b in range(4): w[:, i, b, i, b] = 32
    return weights(rng, w.reshape(N, 128, 2048))
def requantised():
    v = (np.arange(1, 16, 2)[:, None] * 2.0 ** -np.arange(10.0, 22.0)).reshape(-1)
    t = np.zeros((128, len(v), 4), np.float32)
    t[8, :, 0] = v
    t[9, :, 0] = 255 * 2.0 ** -7
    once = decode(mx_ref.quantize(t.reshape(128, -1).astype(BF)))
    again = decode(mx_ref.quantize(once.astype(BF)))
    i = int(np.argmax(np.abs(once - again)[8, ::4]))
    return float(v[i]), float(once[8, 4 * i]), float(again[8, 4 * i])
def planted(rng, m, unit, near, fine=False):
    d = numbers_of(rng)
    p = rng.permutation(8)
    s = p % 2 * 2 - 1
    if not near: m = np.where(s[:, None, None] > 0, m, 4 - m)
    x = d["x"].reshape(N, 8, 16, 3, C, 4)
    x[:, :, 0] = 0
    x[:, :, 8:] = 0
    x[:, :, 0, :, :, 0] = near
    if near: x[:, :, 0, 0, :, 0] = np.where(np.roll(m[:, :, 2], 1, axis=0) == 3, s[:, None] * 2.0 ** 28, 1.0).astype(np.float32).astype(BF)
    for b in range(3): x[:, :, 8, :, :, b] = ((m >> b & 1) * 2.0 ** b * unit).astype(np.float32).astype(BF)
    if fine:
        for g in range(8):
            if p[g] < 4:
                x[:, g, 8] = 0
                x[:, g, 8, :, :, 0] = ((4 + m[:, g]) * 2.0 ** -32).astype(np.float32).astype(BF)
        v, once, again = requantised()
        for h in (5, 7):
            g, j = int(np.argmax(p == h)), int(rng.integers(A))
            x[:, g, 8, :, j] = 0
            x[:, g, 8, 0, j, 0] = BF(min(once, again))
            x[:, g, 8, 1, j, 0] = BF(v)
            x[:, g, 9, 1, j, 0] = BF(255 * 2.0 ** -7)
    u = d["u"].reshape(N, 128, 128, 4)
    u[:, :, ::16] = 0
    k = np.where(rng.permutation(N) < N // 2, 2.0 ** -30, 1.0)
    for g in range(8):
        u[:, 16 * g, 16 * g, 0] = (k * s[g]).astype(np.float32).astype(BF)
        u[:, 16 * g + 8, 16 * g, :3] = (k * (1 if near else s[g])).astype(np.float32).astype(BF)[:, None]
    return {"x": x.reshape(N, 128, 12 * C), "u": u.reshape(N, 128, 512), "v": d["v"], **passing(rng)}
def setup_inputs(rng):
    return {**numbers_of(rng), **weights(rng, f(rng, N, 128, 2048))}
def setup_inputs_counts(rng):
    return planted(rng, marks(rng), 1.0, 0)
def setup_inputs_ties(rng):
    return planted(rng, rng.integers(0, 4, (N, 8, 3, C)), 2.0 ** -24, 0, True)
def setup_inputs_near(rng):
    return planted(rng, marks(rng), 2.0 ** -23, 1)
def setup_inputs_huge(rng):
    d = numbers_of(rng)
    x = 2.0 ** 28 * (1.5 + 0.5 * rng.random((N, 128, 12 * C)))
    x[int(rng.integers(N))] *= 2
    u = d["u"].reshape(N, 128, 128, 4)
    s = np.stack([rng.permutation(8) % 2 * 2.0 - 1.0 for r in range(N)])
    u[:, :, ::16] = (2.0 ** 30 * (0.75 + 0.25 * rng.random((N, 128, 8, 4))) * s[:, None, :, None]).astype(np.float32).astype(BF)
    w = np.zeros((N, 128, 4, 128, 4), np.float32)
    i = np.arange(128)
    for b in range(4): w[:, i, b, i, b] = 32
    return {"x": x.astype(np.float32).astype(BF), "u": u.reshape(N, 128, 512), "v": d["v"], **weights(rng, w.reshape(N, 128, 2048).astype(BF))}
def setup_inputs_spread(rng):
    d = setup_inputs(rng)
    d["x"] = big(wide(rng, N, 128, 12 * C, cols=6), 1)
    return d
def check_inputs(d):
    b = []
    for k in ("x", "u", "v"):
        a = np.abs(d[k].astype(np.float32))
        if not (np.isfinite(a).all() and ((a == 0) | (a >= 2.0 ** -30) & (a <= 2.0 ** 30)).all()): b.append("a value of " + k)
    return b
def reference(x, u, v, wc, ws):
    lay = [pk(wc[r], ws[r]) for r in range(N)]
    qu = [mx_ref.quantize(u[r]) for r in range(N)]
    level = [[np.ascontiguousarray(cut(x[r], k, 4 * C)) for k in range(3)] for r in range(N)]
    first = [mx_ref.matmul(qu[r], mx_ref.quantize(level[r][0]))[::16] for r in range(N)]
    y, ol = np.zeros((N, 128, C), np.float32), np.zeros((N, 8, R * A), np.float32)
    oc, osc = np.zeros((N, 128, 4 * C), np.uint8), np.zeros((N, 16, C), np.uint8)
    for t in range(R):
        held = [[mx_ref.quantize(level[r][k]) for k in (1, 2)] for r in range(N)]
        for r in range(N):
            log = [decode(q).astype(BF) for q in held[(r - 1) % N]]
            s = [mx_ref.matmul(qu[r], mx_ref.quantize(g))[::16] for g in log]
            p = [first[r], mx_ref.matmul(qu[r], held[r][0])[::16]]
            c = slots(s, p)
            ol[r][:, A * t:A * t + A] = c
            e = np.where(c < 0, -1, c % C)
            for k in (0, 1):
                z = (gcols(level[r][k], e).astype(np.float32) + gcols(log[k], e).astype(np.float32)) * np.float32(0.5)
                q = mx_ref.quantize(z.astype(BF))
                made = tile([np.maximum(mx_ref.matmul(pick(lay[r], np.arange(128 * a, 128 * a + 128)), q), np.float32(0.0)) * np.float32(0.03125) for a in range(4)])
                level[r][k + 1] = replaced(level[r][k + 1], np.where(c < C * k + C, e, -1), made)
    for r in range(N):
        q = mx_ref.quantize(level[r][2])
        y[r] = mx_ref.matmul(mx_ref.quantize(v[r]), q)
        oc[r], osc[r] = emit(q)
    return {"y": y, "ol": ol, "oc": oc, "osc": osc}

@@ -1,0 +1,483 @@
+from concourse.mybir import dt, AluOpType, ActivationFunctionType
+
+C, A, R = 256, 144, 3
+D = C // 2
+PL = 416
+XW = 400
+OFF = C - A
+BF, F32, F16, I32, U16, QC, QS = "bfloat16", "float32", "float16", "int32", "uint16", "float8_e4m3fn_x4", "uint8"
+
+SCRATCH = {"psx": ("psum", [128, 2048], F32), "psy": ("psum", [128, 2048], F32)}
+
+
+def _bufs(names, n, d):
+    for name in names.split():
+        SCRATCH[name] = ("sbuf", [128, n], d)
+
+
+def _pairs(names, n):
+    for name in names.split():
+        _bufs(name + "c", n, QC)
+        _bufs(name + "s", n, QS)
+
+
+_bufs("h0 h1_0 h1_1 h1_2 h2", 4 * C, BF)
+_bufs("gw_0 gw_1 gw_2", 4 * A + 4 * C, BF)
+_bufs("hw", R * 4 * A + 4 * C, BF)
+_bufs("g1 m0_0 m0_1 m0_2", 4 * C + 16, BF)
+_bufs("ut vt", 512, BF)
+_pairs("uraw uq vq", 128)
+_pairs("wq eq", 512)
+_bufs("et", 2048, BF)
+_pairs("q0 q1_0 qh q2_0 q2_3 l1_0 l2_0 gq0 gq1", C)
+_pairs("zq0 zq1 q1_1 q1_2 l1_1 l1_2 q2_1 q2_2 l2_1 l2_2", A)
+_bufs("p0s p1s mx1 thr0 ysb", C, F32)
+_bufs("l0 kk lanes km", C, BF)
+_bufs("ff", 2 * C + 16, F16)
+_bufs("yy hd k16", 2 * C, F16)
+_bufs("k16g k4 k4a h4", A, F16)
+_bufs("km4", A, BF)
+_bufs("h16", A, F32)
+_bufs("wi aa ma c2", 32, I32)
+_bufs("mb pi mn ix iy", 16, I32)
+_bufs("list2 cl uoff", 16, U16)
+_bufs("e4", A // 4, U16)
+_bufs("l4 lb", 64, U16)
+_bufs("il_0 il_1 il_2 li_1 li_2", 32, U16)
+_bufs("col jq jj i2c cv y255 u1 u2 vv s1 s2", 16, F32)
+_bufs("xx", R * XW, BF)
+_bufs("table", 2 * C + 16, F32)
+_bufs("idv", 128, F32)
+_bufs("w1 w2", 4 * PL, BF)
+_bufs("z0 z1 g1e t0", 4 * A, BF)
+_bufs("olr", R * A, F32)
+
+SEMAPHORES = ["cv", "ca", "cp", "cg", "sent0", "sent1"] + ["arr%d" % k for k in range(3 * R)] + ["d%d" % k for k in range(26)]
+
+PLAN = {
+    "z0v": 18, "g1v": 12, "split0": 1,
+    "rx0": "a0 a1 ev1 m1 a2 ea0 m0 a3 d0 ea2 d2 m2 ea3 q0 m3 d1 fa0 s0 c0 fa2 c1 kv0 fa1 d3 fa3 p0 p1 c3 l2 l0 l3 l1",
+    "mid": "rv0 z0 ra1 ra2 z1 ra3 na1 nv0 nv2 nv3 z2 o1 z3 ha0 qz a3 a2 a0 hv3 ha1 ta3 a1 tv0 ha2 tv1 tv2 o2 lb qh K0 vq W0 ev3 ea2 W1 d2 K1 "
+           "ev0 Pv0 ea1 d1 d0 wv1 d3 wa3 wv0 W2 wa2 q0 fa2 fv0 fa1 fv3 ua2 ma ua5 uv0 ua3 ua7 s0 uv1 c0 ua6 c1 p0 kv0 ua4 p1 K2 c3 l2 l0 l3 l1",
+    "end": "ra0 rv1 z0 z1 ra2 ra3 z2 z3 W0 qz ta1 W1 K0 W2 tv2 tv3 ta0 K1 Gv2 Ga0 Ga3 K2 Gv1 xx",
+}
+
+
+def rank_program(g, core, T, topo):
+    rank = T.rank_of(core)
+    if rank is None:
+        return
+    n_ranks = len(T.cores)
+    nxt, prv = T.cores[(rank + 1) % n_ranks], T.cores[(rank - 1) % n_ranks]
+    rid, pid, _se = topo.addr(nxt)
+    mask = topo.mask(core, nxt)
+    n_out, n_in = len(topo.engines(core, nxt)), len(topo.engines(prv, core))
+    Q = {"v": g.vector, "a": g.scalar, "p": g.tensor, "g": g, "s": g.sync}
+    OP, AF = AluOpType, ActivationFunctionType
+    ops = []
+    sent = {"sent0": 0, "sent1": 0}
+
+    def V(name, a=0, b=None, s=1):
+        return (name, a, SCRATCH[name][1][1] if b is None else b, s)
+
+    def ap(v):
+        if not isinstance(v, tuple):
+            return v
+        if len(v) == 2:
+            return ap(v[0]).indirect(ap(v[1]))
+        return T[v[0]][:, v[1]:v[2]] if v[3] == 1 else T[v[0]][:, v[1]:v[2]:v[3]]
+
+    def flat(vs):
+        out = []
+        for v in vs:
+            if isinstance(v, tuple):
+                out += list(v) if len(v) == 2 else [v]
+        return out
+
+    def op(q, fn, w, r, kind="c", pre=None, sem=None):
+        ops.append({"q": q, "fn": fn, "w": flat(w), "r": flat(r), "kind": kind, "pre": pre, "sem": sem})
+
+    def ts(o, i, s1, s2, o0, o1=None):
+        if o1 is None:
+            op("v", lambda: g.vector.tensor_scalar(ap(o), ap(i), ap(s1), None, o0), [o], [i, s1])
+        else:
+            op("v", lambda: g.vector.tensor_scalar(ap(o), ap(i), ap(s1), ap(s2), o0, o1), [o], [i, s1, s2])
+
+    def tt(o, a, b, o0):
+        op("v", lambda: g.vector.tensor_tensor(ap(o), ap(a), ap(b), o0), [o], [a, b])
+
+    def cp(o, i):
+        if len(o) == 2:
+            op("v", lambda: g.vector.tensor_copy(ap(o), ap(i)), [o[0]], [i, o[1]])
+        else:
+            op("v", lambda: g.vector.tensor_copy(ap(o), ap(i)), [o], [i])
+
+    def scan(o, a, b, init, o0, o1):
+        op("v", lambda: g.vector.tensor_tensor_scan(ap(o), ap(a), ap(b), init, o0, o1), [o], [a, b])
+
+    def fill(o, c):
+        op("v", lambda: g.vector.memset(ap(o), c), [o], [])
+
+    def act(o, i, f, scale=1.0):
+        op("a", lambda: g.scalar.activation(ap(o), ap(i), f, scale=scale), [o], [i])
+
+    def move(q, o, i, scale=1.0):
+        if q == "a":
+            act(o, i, AF.Copy, scale)
+        elif scale == 1.0:
+            cp(o, i)
+        else:
+            ts(o, i, scale, None, OP.mult)
+
+    def relu(q, o, i, scale):
+        if q == "a":
+            act(o, i, AF.Relu, scale)
+        else:
+            ts(o, i, 0.0, scale, OP.max, OP.mult)
+
+    def iota(o, pat, base, cm):
+        if SCRATCH[o[0]][2] == I32:
+            op("g", lambda: g.iota(ap(o), pat, base, cm), [o], [])
+        else:
+            op("g", lambda: g.iota(ap(o), pat, base, cm, allow_small_or_imprecise_dtypes=True), [o], [])
+
+    def quant(p, i, a=0, b=None):
+        c, s = V(p + "c", a, b), V(p + "s", a, b)
+        op("v", lambda: g.vector.quantize_mx(ap(c), ap(s), ap(i)), [c, s], [i])
+
+    def mm(ps, bank, wp, wa, xp, a=0, b=None):
+        wc, ws, xc, xs = V(wp + "c", wa, wa + 128), V(wp + "s", wa, wa + 128), V(xp + "c", a, b), V(xp + "s", a, b)
+        o = V(ps, 512 * bank, 512 * bank + xc[2] - xc[1])
+        op("p", lambda: g.tensor.matmul_mx(ap(o), ap(wc), ap(ws), ap(xc), ap(xs), True, True), [o], [wc, ws, xc, xs])
+
+    def P(ps, bank, n):
+        return V(ps, 512 * bank, 512 * bank + n)
+
+    def dma(q, fn, w, r, pre=None):
+        op(q, fn, w, r, kind="d", pre=pre)
+
+    def remote(src, dst, k, s):
+        cast = (lambda x: x.bitcast(dt.uint8)) if SCRATCH[src[0]][2] == QC else (lambda x: x)
+        sent[s] += n_out
+        op("g", lambda: g.remote_dma(cast(ap(dst)), cast(ap(src)), T.sem["arr%d" % k], T.sem[s], pid, rid, mask), [], [src], kind="r")
+
+    def send(src, dst, k, s):
+        remote(V(src + "c"), V(dst + "c"), k, s)
+        remote(V(src + "s"), V(dst + "s"), k, s)
+
+    def arrive(views, k, calls):
+        op(None, None, views, [], kind="x", sem=("arr%d" % k, calls * n_in))
+
+    def col(k):
+        return V("col", k, k + 1)
+
+    def G0(t, a=0, s=1):
+        return V("gw_%d" % t, 4 * A + a, 4 * A + 4 * C, s)
+
+    def T1(t, a=0, s=1):
+        return V("hw", 4 * A * (R - 1 - t) + a, 4 * A * (R - t), s)
+
+    def play(plan, calls):
+        for w in plan.split():
+            if w in calls:
+                calls[w]()
+            elif len(w) == 2:
+                calls[w[0]](int(w[1]))
+            else:
+                calls[w[0]](w[1], int(w[2]))
+
+    split = PLAN["split0"]
+    h2x = V("hw", R * 4 * A)
+    if split:
+        dma("s", lambda: g.sync.dma_start(T.h1_0[:, 0:2 * C], T.x[:, 4 * C:6 * C]), [V("h1_0", 0, 2 * C)], [])
+        dma("s", lambda: g.sync.dma_start(T.h1_0[:, 2 * C:4 * C], T.x[:, 6 * C:8 * C]), [V("h1_0", 2 * C, 4 * C)], [])
+    else:
+        dma("s", lambda: g.sync.dma_start(T.h1_0[:], T.x[:, 4 * C:8 * C]), [V("h1_0")], [])
+    dma("s", lambda: g.sync.dma_start(ap(h2x), T.x[:, 8 * C:12 * C]), [h2x], [])
+    dma("s", lambda: g.sync.dma_start(T.ut[:], T.u[:]), [V("ut")], [])
+    dma("s", lambda: g.sync.dma_start(T.h0[:], T.x[:, 0:4 * C]), [V("h0")], [])
+    dma("s", lambda: g.sync.dma_start(T.wqc[:].bitcast(dt.uint8), T.wc[:]), [V("wqc")], [], pre=("sent0", (4 + split) * n_out))
+    dma("s", lambda: g.sync.dma_start(T.wqs[:], T.ws[:]), [V("wqs")], [])
+
+    iota(V("pi", 0, 1), [[0, 1]], 0, 1)
+    iota(V("idv"), [[1, 128]], 0, -1)
+    iota(V("jq"), [[16, 16]], 0, 0)
+    iota(V("km"), [[0, 16], [1, 16]], 0, 0)
+    iota(V("km4"), [[0, A // 4], [1, 4]], 0, 0)
+    fill(V("et"), 0.0)
+    ts(V("pi", 1, 2), V("pi", 0, 1), 15, None, OP.bitwise_and)
+    ts(V("pi", 2, 3), V("pi", 0, 1), 2, 3, OP.arith_shift_right, OP.bitwise_and)
+    ts(V("pi", 3, 4), V("pi", 0, 1), 3, None, OP.bitwise_and)
+    for b in range(4):
+        ts(V("et", 512 * b + b, 512 * b + 512, 4), V("idv"), 0.0, None, OP.is_equal)
+    cp(V("col", 0, 3), V("pi", 1, 4))
+    cp(V("uoff", 0, 8), V("jq", 0, 8))
+
+    if split:
+        quant("q1_0", V("h1_0", 0, 2 * C), 0, D)
+        remote(V("q1_0c", 0, D), V("l1_0c", 0, D), 0, "sent0")
+        quant("q1_0", V("h1_0", 2 * C, 4 * C), D, C)
+        remote(V("q1_0c", D, C), V("l1_0c", D, C), 0, "sent0")
+        remote(V("q1_0s"), V("l1_0s"), 0, "sent0")
+    else:
+        quant("q1_0", V("h1_0"))
+        send("q1_0", "l1_0", 0, "sent0")
+    quant("eq", V("et"))
+    quant("q2_0", h2x)
+    send("q2_0", "l2_0", 1, "sent0")
+    iota(V("table", 0, 2 * C), [[1, 2 * C]], 0, 0)
+
+    ts(col(3), col(1), -2048.0, 6144.0, OP.mult, OP.add)
+    ts(col(5), col(0), -512.0, 7680.0, OP.mult, OP.add)
+    ts(V("jj"), V("jq"), col(0), None, OP.add)
+    fill(V("ff", 0, 16), 0.0)
+    quant("uraw", V("ut"))
+    tt(col(4), col(3), col(2), OP.add)
+    ts(col(6), col(5), float(A), None, OP.add)
+    op("v", lambda: g.vector.tensor_copy(T.uqc[:].bitcast(dt.uint32), T.urawc[:].bitcast(dt.uint32).indirect(T.uoff[:, 0:8])),
+       [V("uqc")], [V("urawc"), V("uoff", 0, 8)])
+    op("v", lambda: g.vector.tensor_copy(T.uqs[:], T.uraws[:].indirect(T.uoff[:, 0:8])), [V("uqs")], [V("uraws"), V("uoff", 0, 8)])
+    ts(V("c2", 0, 16), V("jj"), float(C), None, OP.add)
+    ts(V("c2", 16, 32), V("jj"), float(C), None, OP.add)
+    ts(V("i2c"), V("jj"), 2.0, 2.0 * OFF - 1, OP.mult, OP.add)
+    ts(V("cv"), V("jj"), col(6), None, OP.subtract)
+    quant("q0", V("h0"))
+    mm("psy", 1, "uq", 0, "q1_0")
+    mm("psy", 2, "uq", 0, "q0")
+    move("a", V("p1s"), P("psy", 1, C))
+    move("a", V("p0s"), P("psy", 2, C))
+    for k in range(2):
+        ts(V("k16", C * k, C * k + C), V("km"), col(0), 16384.0, OP.is_equal, OP.mult)
+    ts(V("k4a"), V("km4"), col(1), 4096.0, OP.is_equal, OP.mult)
+    fill(V("xx"), float(C))
+    ts(V("k16g"), V("k16", 0, A), -512.0, None, OP.add)
+    ts(V("k4"), V("k4a"), -512.0, None, OP.add)
+    cp(V("lanes"), V("table", 0, C))
+    fill(V("table", 2 * C, 2 * C + 16), -1.0)
+    fill(V("g1", 4 * C, 4 * C + 16), 0.0)
+    for t in range(R):
+        fill(V("m0_%d" % t, 4 * C, 4 * C + 16), 0.0)
+    for a in range(4):
+        fill(V("w1", PL * a + A + C, PL * a + PL), 0.0)
+
+    def logs(t):
+        n = A if t else C
+        s0 = P("psx", 0, C)
+        m0 = V("m0_%d" % t, 0, 4 * C)
+        arrive([V("l1_%dc" % t), V("l1_%ds" % t)], 3 * t, 2 + (split if t == 0 else 0))
+        arrive([V("l2_%dc" % t), V("l2_%ds" % t)], 3 * t + 1, 2)
+        if t:
+            arrive([V("li_%d" % t)], 3 * t + 2, 1)
+
+        def lists_b():
+            for b in range(4):
+                ts(V("lb", 16 * b, 16 * b + 16), V("li_%d" % t, 0, 16), 4.0, float(b), OP.mult, OP.add)
+
+        def score1(h):
+            quant("gq1", V("g1", 2 * C * h, 2 * C * h + 2 * C), D * h, D * h + D)
+            mm("psy", h, "uq", 0, "gq1", D * h, D * h + D)
+
+        def late(k):
+            lv, lo, hi = k // 2, D * (k % 2), D * (k % 2) + D
+            tt(V("ff", 16 + C * lv + lo, 16 + C * lv + hi), P("psy", k % 2, D), V("mx1" if lv else "thr0", lo, hi), OP.is_gt if lv else OP.is_le)
+
+        def update(q, k):
+            b, h = k % 4, k // 4
+            move(q, V("g1", 2 * C * h + b, 2 * C * h + 2 * C, 4), (V("w2", PL * b, PL * b + A + C), V("li_%d" % t, 16 + 8 * h, 24 + 8 * h)))
+
+        return {
+            "a": lambda b: mm("psx", b, "eq", 128 * b, "l1_%d" % t),
+            "e": lambda q, b: move(q, V("gw_%d" % (t - 1), b, 4 * A, 4) if t else G0(t, b, 4), P("psx", b, n)),
+            "lb": lists_b,
+            "w": lambda q, b: move(q, G0(t, b, 4), (V("gw_%d" % (t - 1)), V("lb", 16 * b, 16 * b + 16))),
+            "m": lambda b: tt(V("m0_0", b, 4 * C, 4), P("psx", b, C), V("h0", b, 4 * C, 4), OP.add),
+            "ma": lambda: dma("g", lambda: g.dma_start(ap(m0), ap(G0(t)), accum_op=OP.add), [m0], [G0(t), m0]),
+            "q0": lambda: quant("gq0", G0(t)),
+            "s0": lambda: mm("psx", 0, "uq", 0, "gq0"),
+            "d": lambda b: mm("psy", b, "eq", 128 * b, "l2_%d" % t),
+            "f": lambda q, b: move(q, V("w2", PL * b, PL * b + A) if t else V("g1", b, 4 * C, 4), P("psy", b, n)),
+            "u": update, "p": score1, "l": late,
+            "c0": lambda: tt(V("l0"), s0, V("p0s"), OP.is_gt),
+            "c1": lambda: tt(V("mx1"), s0, V("p1s"), OP.max),
+            "k": lambda q, _k: ts(V("kk"), V("l0"), -0.5, 2.0 ** 91, OP.add, OP.mult),
+            "c3": lambda: tt(V("thr0"), s0, V("kk"), OP.min),
+        }
+
+    def replay(t):
+        def replay1():
+            quant("zq1", V("z1"))
+            for a in range(4):
+                mm("psy", a, "wq", 128 * a, "zq1")
+
+        def out1():
+            quant("q1_%d" % (t + 1), V("t0"))
+            send("q1_%d" % (t + 1), "l1_%d" % (t + 1), 3 * t + 3, "sent1")
+
+        def out2():
+            quant("q2_%d" % (t + 1), T1(t))
+            send("q2_%d" % (t + 1), "l2_%d" % (t + 1), 3 * t + 4, "sent1")
+
+        def own1():
+            quant("qh", V("h1_%d" % (t + 1)))
+            mm("psy", 3, "uq", 0, "qh")
+
+        def keys():
+            ts(V("u1", 0, 9), V("u2", 0, 9), 0.5, col(5), OP.mult, OP.add)
+            tt(V("s2", 0, 9), V("h16", 15, A, 16), V("u1", 0, 9), OP.add)
+
+        def where0():
+            if t:
+                tt(V("mn"), V("aa", 0, 16), V("aa", 16, 32), OP.min)
+
+        def where1():
+            if t:
+                tt(V("ix"), V("mn"), V("iy"), OP.min)
+
+        def where2():
+            if t < R - 1:
+                ts(V("iy"), V("ix" if t else "mb"), float(A), None, OP.add)
+            else:
+                for a in range(4):
+                    ts(V("l4", 16 * a, 16 * a + 16), V("ix"), 4.0, a - 4.0 * OFF, OP.mult, OP.add)
+
+        def once():
+            if t == 0:
+                quant("vq", V("vt"))
+
+        def outputs():
+            quant("q2_3", V("h2"))
+            mm("psx", 0, "vq", 0, "q2_3")
+            dma("s", lambda: g.sync.dma_start(T.oc[:], T.q2_3c[:].bitcast(dt.uint8)), [], [V("q2_3c")])
+            move("v", V("ysb"), P("psx", 0, C))
+            dma("s", lambda: g.sync.dma_start(T.y[:], T.ysb[:]), [], [V("ysb")])
+
+        return {
+            "r": lambda q, a: relu(q, V("w1", PL * a, PL * a + A), P("psx", a, A), 2.0 ** -6),
+            "z": lambda a: tt(V("z1", a, 4 * A, 4), (V("w1", PL * a, PL * a + PL), V("list2", 0, 9)), V("g1e", a, 4 * A, 4), OP.add),
+            "n": lambda q, a: move(q, V("t0", a, 4 * A, 4), V("w1", PL * a, PL * a + A), 2.0),
+            "qz": replay1,
+            "h": lambda q, a: move(q, V("h1_%d" % (t + 1), a, 4 * C, 4), (V("w1", PL * a, PL * a + A + C), V("il_%d" % t, 0, 16)), 2.0),
+            "t": lambda q, a: relu(q, T1(t, a, 4), P("psy", a, A), 2.0 ** -5),
+            "o1": out1, "o2": out2, "qh": own1,
+            "P": lambda q, _k: move(q, V("p1s"), P("psy", 3, C)),
+            "K0": keys, "K1": lambda: cp(V("cl", 0, 9), V("s2", 0, 9)),
+            "K2": lambda: move("a", V("olr", A * t, A * t + A), (V("table"), V("cl", 0, 9))),
+            "W0": where0, "W1": where1, "W2": where2, "vq": once,
+            "G": lambda q, a: move(q, V("h2", a, 4 * C, 4), (V("hw"), V("l4", 16 * a, 16 * a + 16))),
+            "xx": outputs,
+        }
+
+    play(PLAN["rx0"], logs(0))
+    for t in range(R):
+        last = t == R - 1
+        for a in range(4):
+            move("a", V("w1", PL * a + A, PL * a + A + C), V("h1_%d" % t, a, 4 * C, 4), 0.5)
+        if not last:
+            for a in range(4):
+                move("a", V("w2", PL * a + A, PL * a + A + C), V("g1", a, 4 * C, 4))
+            dma("s", lambda t=t: g.sync.dma_start(T["m0_%d" % (t + 1)][:, 0:4 * C], T.x[:, 0:4 * C]), [V("m0_%d" % (t + 1), 0, 4 * C)],
+                [V("m0_%d" % t, 0, 4 * C)])
+        if t == 0:
+            dma("s", lambda: g.sync.dma_start(T.vt[:], T.v[:]), [V("vt")], [])
+        i2 = V("il_%d" % t, 16, 32)
+        scan(V("yy"), V("ff", 15, 15 + 2 * C), V("ff", 16, 16 + 2 * C), 2.0 * OFF - 1, OP.add, OP.add)
+        scan(V("hd"), V("k16"), V("yy"), 0.0, OP.add, OP.min)
+        cp(V("y255", 0, 1), V("yy", C - 1, C))
+        ts(V("wi"), V("hd", 15, 2 * C, 16), 2049.0, None, OP.mult)
+        ts(V("u2", 0, 9), V("i2c", 0, 9), V("y255", 0, 1), 512.0, OP.is_ge, OP.mult)
+        ts(V("aa"), V("wi"), 1, 255 + 1024 + 2 ** 19, OP.arith_shift_right, OP.bitwise_and)
+        tt(V("vv", 0, 9), V("u2", 0, 9), V("cv", 0, 9), OP.add)
+        tt(V("ma"), V("aa"), V("c2"), OP.min)
+        tt(V("mb"), V("ma", 0, 16), V("ma", 16, 32), OP.min)
+        if not last:
+            ts(V("il_%d" % t, 0, 16), V("ma", 0, 16), -float(OFF), None, OP.add)
+        ts(i2, V("mb"), -float(OFF), None, OP.add)
+        if not last:
+            remote(V("il_%d" % t), V("li_%d" % (t + 1)), 3 * t + 5, "sent1")
+        xw, xs = V("xx", XW * t, XW * t + XW), V("xx", XW * t, XW * t + A)
+        cp((xw, i2), V("lanes"))
+        scan(V("h4"), V("k4"), xs, 0.0, OP.add, OP.min)
+        scan(V("h16"), V("k16g"), xs, 0.0, OP.add, OP.min)
+        ts(V("e4"), V("h4", 3, A, 4), 4.0, col(4), OP.mult, OP.add)
+        zv, gv = PLAN["z0v"], PLAN["g1v"]
+        move("a", V("z0", 16 * zv, 4 * A), (V("m0_%d" % t), V("e4", zv)), 0.5)
+        move("v", V("z0", 0, 16 * zv), (V("m0_%d" % t), V("e4", 0, zv)), 0.5)
+        tt(V("s1", 0, 9), V("h16", 15, A, 16), V("vv", 0, 9), OP.min)
+        quant("zq0", V("z0"))
+        for a in range(4):
+            mm("psx", a, "wq", 128 * a, "zq0")
+        move("a", V("g1e", 16 * gv, 4 * A), (V("g1"), V("e4", gv)), 0.5)
+        ts(V("list2", 0, 9), V("s1", 0, 9), col(6), None, OP.add)
+        move("v", V("g1e", 0, 16 * gv), (V("g1"), V("e4", 0, gv)), 0.5)
+        calls = replay(t)
+        if not last:
+            calls.update(logs(t + 1))
+        play(PLAN["end" if last else "mid"], calls)
+
+    dma("a", lambda: g.scalar.dma_start(T.ol[:], T.olr[0:128:16, :]), [], [V("olr")])
+    for k in range(4):
+        dma("a", lambda k=k: g.scalar.dma_start(T.osc[4 * k:4 * k + 4, :], T.q2_3s[32 * k:32 * k + 4, :]), [], [V("q2_3s")])
+
+    def bits(v):
+        n = (v[2] - v[1] + v[3] - 1) // v[3]
+        return ((1 << (n * v[3])) - 1) // ((1 << v[3]) - 1) << v[1]
+
+    def banks(v):
+        return ((1 << ((v[2] - 1) // 512 + 1)) - 1) >> (v[1] // 512) << (v[1] // 512)
+
+    touch = {}
+    known = {q: 0 for q in Q}
+    ran = {q: 0 for q in Q}
+    waited = set()
+    for j, o in enumerate(ops):
+        deps = set()
+        for wr, vs in ((True, o["w"]), (False, o["r"])):
+            for v in vs:
+                m, bk = bits(v), banks(v) if SCRATCH[v[0]][0] == "psum" else 0
+                for (i, mi, bi, wi) in touch.get(v[0], []):
+                    if i != j and (((wr or wi) and mi & m) or (bi & bk and ops[i]["q"] != o["q"])):
+                        deps.add(i)
+                touch.setdefault(v[0], []).append((j, m, bk, wr))
+        q = o["q"]
+        o["waits"] = []
+        if q is None:
+            o["done"] = 1 << j
+            continue
+        for i in sorted(deps, reverse=True):
+            if not known[q] >> i & 1:
+                o["waits"].append(i)
+                waited.add(i)
+                known[q] |= ops[i]["done"]
+        if o["kind"] == "c":
+            ran[q] |= 1 << j
+            o["done"] = known[q] | ran[q]
+        else:
+            o["done"] = known[q] | 1 << j
+    count = {q: 0 for q in Q}
+    n_d = 0
+    tail = []
+    for j, o in enumerate(ops):
+        if o["kind"] == "c" and j in waited:
+            count[o["q"]] += 1
+            o["sem"] = ("c" + o["q"], count[o["q"]])
+        elif o["kind"] == "d":
+            o["sem"] = ("d%d" % n_d, 16)
+            n_d += 1
+            if j not in waited:
+                tail.append(o)
+    for j, o in enumerate(ops):
+        if o["q"] is None:
+            continue
+        e = Q[o["q"]]
+        if o["pre"] is not None:
+            e.wait_ge(T.sem[o["pre"][0]], o["pre"][1])
+        for i in o["waits"]:
+            e.wait_ge(T.sem[ops[i]["sem"][0]], ops[i]["sem"][1])
+        ins = o["fn"]()
+        if o["kind"] == "d":
+            ins.then_inc(T.sem[o["sem"][0]], 16)
+        elif o["kind"] == "c" and j in waited:
+            ins.then_inc(T.sem[o["sem"][0]], 1)
+    g.wait_ge(T.sem.sent1, sent["sent1"])
+    for o in tail:
+        g.wait_ge(T.sem[o["sem"][0]], 16)

@@ -3,8 +3,7 @@ from concourse.mybir import dt, AluOpType, ActivationFunctionType
 C, A, R = 256, 144, 3
 D = C // 2
 PL = 416
-XW = 400
-OFF = C - A
+XW = 528
 BF, F32, F16, I32, U16, QC, QS = "bfloat16", "float32", "float16", "int32", "uint16", "float8_e4m3fn_x4", "uint8"
 
 SCRATCH = {"psx": ("psum", [128, 2048], F32), "psy": ("psum", [128, 2048], F32)}
@@ -28,23 +27,25 @@ _bufs("g1 m0_0 m0_1 m0_2", 4 * C + 16, BF)
 _bufs("ut vt", 512, BF)
 _pairs("uraw uq vq", 128)
 _pairs("wq eq", 512)
-_bufs("et", 2048, BF)
+_bufs("et", 516, BF)
 _pairs("q0 q1_0 qh q2_0 q2_3 l1_0 l2_0 gq0 gq1", C)
 _pairs("zq0 zq1 q1_1 q1_2 l1_1 l1_2 q2_1 q2_2 l2_1 l2_2", A)
 _bufs("p0s p1s mx1 thr0 ysb", C, F32)
 _bufs("l0 kk lanes km", C, BF)
 _bufs("ff", 2 * C + 16, F16)
-_bufs("yy hd k16", 2 * C, F16)
+_bufs("yy hd hf k16 kf", 2 * C, BF)
 _bufs("k16g k4 k4a h4", A, F16)
 _bufs("km4", A, BF)
+_bufs("kg", C, BF)
 _bufs("h16", A, F32)
-_bufs("wi aa ma c2", 32, I32)
-_bufs("mb pi mn ix iy", 16, I32)
-_bufs("list2 cl uoff", 16, U16)
+_bufs("pre aa ab mn ma c2 cn", 32, F32)
+_bufs("ix iy", 16, F32)
+_bufs("pi", 16, I32)
+_bufs("list2 cl uoff i2", 16, U16)
 _bufs("e4", A // 4, U16)
 _bufs("l4 lb", 64, U16)
-_bufs("il_0 il_1 il_2 li_1 li_2", 32, U16)
-_bufs("col jq jj i2c cv y255 u1 u2 vv s1 s2", 16, F32)
+_bufs("il_0 il_1 li_1 li_2", 32, U16)
+_bufs("col jq jj cv u1 u2 vv s1 s2", 16, F32)
 _bufs("xx", R * XW, BF)
 _bufs("table", 2 * C + 16, F32)
 _bufs("idv", 128, F32)
@@ -52,14 +53,13 @@ _bufs("w1 w2", 4 * PL, BF)
 _bufs("z0 z1 g1e t0", 4 * A, BF)
 _bufs("olr", R * A, F32)
 
-SEMAPHORES = ["cv", "ca", "cp", "cg", "sent0", "sent1"] + ["arr%d" % k for k in range(3 * R)] + ["d%d" % k for k in range(26)]
+SEMAPHORES = ["cv", "ca", "cp", "cg", "sent0", "sent1"] + ["arr%d" % k for k in range(3 * R)] + ["d%d" % k for k in range(30)]
 
 PLAN = {
-    "z0v": 18, "g1v": 12, "split0": 1,
-    "rx0": "a0 a1 ev1 m1 a2 ea0 m0 a3 d0 ea2 d2 m2 ea3 q0 m3 d1 fa0 s0 c0 fa2 c1 kv0 fa1 d3 fa3 p0 p1 c3 l2 l0 l3 l1",
-    "mid": "rv0 z0 ra1 ra2 z1 ra3 na1 nv0 nv2 nv3 z2 o1 z3 ha0 qz a3 a2 a0 hv3 ha1 ta3 a1 tv0 ha2 tv1 tv2 o2 lb qh K0 vq W0 ev3 ea2 W1 d2 K1 "
-           "ev0 Pv0 ea1 d1 d0 wv1 d3 wa3 wv0 W2 wa2 q0 fa2 fv0 fa1 fv3 ua2 ma ua5 uv0 ua3 ua7 s0 uv1 c0 ua6 c1 p0 kv0 ua4 p1 K2 c3 l2 l0 l3 l1",
-    "end": "ra0 rv1 z0 z1 ra2 ra3 z2 z3 W0 qz ta1 W1 K0 W2 tv2 tv3 ta0 K1 Gv2 Ga0 Ga3 K2 Gv1 xx",
+    "acc0": 0, "z0v": 18, "g1v": 10,
+    "rx0": "a1 a3 a2 a0 d2 d3 ev1 ea3 ev0 d1 ea2 d0 q0 fa2 fa3 fv1 s0 fa0 c0 p0 p1 c1 ka0 c3 l3 l2 l0 l1",
+    "mid": "M0 sy Oa0 hf sh Oa1 pr M2 aa M3 mb M1 i2 Oa2 Oa3 u2 sc Ba0 Ba3 b0 ld h4 Ba2 h6 e4 b1 Zv vv Ba1 b2 Za qy s1 gv j2 ga rv0 i0 ra1 rv2 ra3 ls nv0 na2 z0 nv3 na1 ha3 z3 o1 z1 ha1 ha2 z2 W1 qz K0 ta0 ta2 tv1 ha0 a0 tv3 a1 a3 o2 ea0 ea1 lb a2 ea2 qh ev3 wv1 d2 wa3 wa2 d1 d0 Pa0 wv0 d3 fa2 W2 vq q0 s0 ma fv1 uv2 fa0 fa3 uv1 uv0 ua5 ua3 ua4 c0 p0 ua7 uv6 c1 p1 ka0 c3 l2 l0 l3 l1 K1 K2",
+    "end": "sy hf Oa1 sh pr u2 Oa0 aa vv mb Oa2 Oa3 i2 sc b0 h4 h6 e4 s1 Zv Za ga j2 b1 qy gv ra0 K0 ra1 z0 z1 ra2 z2 ra3 z3 W1 qz W2 ta0 ta2 tv1 tv3 gv6 ga7 gv5 ga4 x1 ga3 gv1 ga2 gv0 K1 ya1 x0 K2 yv0",
 }
 
 
@@ -75,6 +75,8 @@ def rank_program(g, core, T, topo):
     Q = {"v": g.vector, "a": g.scalar, "p": g.tensor, "g": g, "s": g.sync}
     OP, AF = AluOpType, ActivationFunctionType
     ops = []
+    TAG = [None]
+    PLAN["ops"] = ops
     sent = {"sent0": 0, "sent1": 0}
 
     def V(name, a=0, b=None, s=1):
@@ -95,7 +97,7 @@ def rank_program(g, core, T, topo):
         return out
 
     def op(q, fn, w, r, kind="c", pre=None, sem=None):
-        ops.append({"q": q, "fn": fn, "w": flat(w), "r": flat(r), "kind": kind, "pre": pre, "sem": sem})
+        ops.append({"q": q, "fn": fn, "w": flat(w), "r": flat(r), "kind": kind, "pre": pre, "sem": sem, "tag": TAG[0]})
 
     def ts(o, i, s1, s2, o0, o1=None):
         if o1 is None:
@@ -118,8 +120,9 @@ def rank_program(g, core, T, topo):
     def fill(o, c):
         op("v", lambda: g.vector.memset(ap(o), c), [o], [])
 
-    def act(o, i, f, scale=1.0):
-        op("a", lambda: g.scalar.activation(ap(o), ap(i), f, scale=scale), [o], [i])
+    def act(o, i, f, scale=1.0, bias=0.0):
+        kw = {k: ap(x) for k, x, plain in (("scale", scale, 1.0), ("bias", bias, 0.0)) if x != plain}
+        op("a", lambda: g.scalar.activation(ap(o), ap(i), f, **kw), [o], [i, bias])
 
     def move(q, o, i, scale=1.0):
         if q == "a":
@@ -177,8 +180,9 @@ def rank_program(g, core, T, topo):
     def T1(t, a=0, s=1):
         return V("hw", 4 * A * (R - 1 - t) + a, 4 * A * (R - t), s)
 
-    def play(plan, calls):
+    def play(plan, calls, ph):
         for w in plan.split():
+            TAG[0] = (ph, w if w in calls or len(w) == 2 else w[0] + "_" + w[2])
             if w in calls:
                 calls[w]()
             elif len(w) == 2:
@@ -186,85 +190,86 @@ def rank_program(g, core, T, topo):
             else:
                 calls[w[0]](w[1], int(w[2]))
 
-    split = PLAN["split0"]
     h2x = V("hw", R * 4 * A)
-    if split:
-        dma("s", lambda: g.sync.dma_start(T.h1_0[:, 0:2 * C], T.x[:, 4 * C:6 * C]), [V("h1_0", 0, 2 * C)], [])
-        dma("s", lambda: g.sync.dma_start(T.h1_0[:, 2 * C:4 * C], T.x[:, 6 * C:8 * C]), [V("h1_0", 2 * C, 4 * C)], [])
-    else:
-        dma("s", lambda: g.sync.dma_start(T.h1_0[:], T.x[:, 4 * C:8 * C]), [V("h1_0")], [])
+    h0 = V("m0_0", 0, 4 * C) if PLAN["acc0"] else V("h0")
+    dma("s", lambda: g.sync.dma_start(T.h1_0[:, 0:2 * C], T.x[:, 4 * C:6 * C]), [V("h1_0", 0, 2 * C)], [])
+    dma("s", lambda: g.sync.dma_start(T.h1_0[:, 2 * C:4 * C], T.x[:, 6 * C:8 * C]), [V("h1_0", 2 * C, 4 * C)], [])
     dma("s", lambda: g.sync.dma_start(ap(h2x), T.x[:, 8 * C:12 * C]), [h2x], [])
     dma("s", lambda: g.sync.dma_start(T.ut[:], T.u[:]), [V("ut")], [])
-    dma("s", lambda: g.sync.dma_start(T.h0[:], T.x[:, 0:4 * C]), [V("h0")], [])
-    dma("s", lambda: g.sync.dma_start(T.wqc[:].bitcast(dt.uint8), T.wc[:]), [V("wqc")], [], pre=("sent0", (4 + split) * n_out))
-    dma("s", lambda: g.sync.dma_start(T.wqs[:], T.ws[:]), [V("wqs")], [])
+    dma("s", lambda: g.sync.dma_start(ap(h0), T.x[:, 0:4 * C]), [h0], [])
 
-    iota(V("pi", 0, 1), [[0, 1]], 0, 1)
+    def const(o, c):
+        act(o, V("et", 0, o[2] - o[1]), AF.Identity, 0.0, c)
+
     iota(V("idv"), [[1, 128]], 0, -1)
+    iota(V("pi", 0, 1), [[0, 1]], 0, 1)
     iota(V("jq"), [[16, 16]], 0, 0)
     iota(V("km"), [[0, 16], [1, 16]], 0, 0)
     iota(V("km4"), [[0, A // 4], [1, 4]], 0, 0)
     fill(V("et"), 0.0)
+    fill(V("ff", 0, 16), 0.0)
+    ts(V("et", 3, 515, 4), V("idv"), 0.0, None, OP.is_equal)
     ts(V("pi", 1, 2), V("pi", 0, 1), 15, None, OP.bitwise_and)
     ts(V("pi", 2, 3), V("pi", 0, 1), 2, 3, OP.arith_shift_right, OP.bitwise_and)
     ts(V("pi", 3, 4), V("pi", 0, 1), 3, None, OP.bitwise_and)
     for b in range(4):
-        ts(V("et", 512 * b + b, 512 * b + 512, 4), V("idv"), 0.0, None, OP.is_equal)
+        quant("eq", V("et", 3 - b, 515 - b), 128 * b, 128 * b + 128)
     cp(V("col", 0, 3), V("pi", 1, 4))
     cp(V("uoff", 0, 8), V("jq", 0, 8))
-
-    if split:
-        quant("q1_0", V("h1_0", 0, 2 * C), 0, D)
-        remote(V("q1_0c", 0, D), V("l1_0c", 0, D), 0, "sent0")
-        quant("q1_0", V("h1_0", 2 * C, 4 * C), D, C)
-        remote(V("q1_0c", D, C), V("l1_0c", D, C), 0, "sent0")
-        remote(V("q1_0s"), V("l1_0s"), 0, "sent0")
-    else:
-        quant("q1_0", V("h1_0"))
-        send("q1_0", "l1_0", 0, "sent0")
-    quant("eq", V("et"))
-    quant("q2_0", h2x)
-    send("q2_0", "l2_0", 1, "sent0")
-    iota(V("table", 0, 2 * C), [[1, 2 * C]], 0, 0)
-
     ts(col(3), col(1), -2048.0, 6144.0, OP.mult, OP.add)
     ts(col(5), col(0), -512.0, 7680.0, OP.mult, OP.add)
     ts(V("jj"), V("jq"), col(0), None, OP.add)
-    fill(V("ff", 0, 16), 0.0)
-    quant("uraw", V("ut"))
+    for t in range(R):
+        const(V("xx", XW * t, XW * t + A), float(C))
+        const(V("m0_%d" % t, 4 * C, 4 * C + 16), 0.0)
+    const(V("g1", 4 * C, 4 * C + 16), 0.0)
+    for a in range(4):
+        const(V("w1", PL * a + A + C, PL * a + PL), 0.0)
+
+    quant("q1_0", V("h1_0", 0, 2 * C), 0, D)
+    remote(V("q1_0c", 0, D), V("l1_0c", 0, D), 0, "sent0")
     tt(col(4), col(3), col(2), OP.add)
     ts(col(6), col(5), float(A), None, OP.add)
+    for k in range(2):
+        act(V("c2", 16 * k, 16 * k + 16), V("jj"), AF.Identity, 1.0, float(A))
+    const(V("cn", 0, 16), 2.0 * XW)
+    act(V("cn", 16, 32), V("jj"), AF.Identity, 1.0, XW - C - 8.0)
+    ts(V("kg"), V("km"), col(0), None, OP.is_gt)
+    quant("q1_0", V("h1_0", 2 * C, 4 * C), D, C)
+    remote(V("q1_0c", D, C), V("l1_0c", D, C), 0, "sent0")
+    remote(V("q1_0s"), V("l1_0s"), 0, "sent0")
+    ts(V("k16", 0, C), V("km"), col(0), 16384.0, OP.is_equal, OP.mult)
+    ts(V("cv"), V("jj"), col(6), None, OP.subtract)
+    ts(V("k4a"), V("km4"), col(1), 4096.0, OP.is_equal, OP.mult)
+    tt(V("kf", 0, C), V("kg"), V("k16", 0, C), OP.add)
+    move("a", V("k16", C, 2 * C), V("k16", 0, C))
+    move("a", V("kf", 15, C, 16), V("kf", 15, C, 16), -0.25)
+    move("a", V("kf", C, 2 * C), V("kf", 0, C))
+    ts(V("k16g"), V("k16", 0, A), -512.0, None, OP.add)
+    ts(V("k4"), V("k4a"), -512.0, None, OP.add)
+    quant("q2_0", h2x)
+    send("q2_0", "l2_0", 1, "sent0")
+    dma("s", lambda: g.sync.dma_start(T.wqc[:].bitcast(dt.uint8), T.wc[:]), [V("wqc")], [], pre=("sent0", 5 * n_out))
+    dma("s", lambda: g.sync.dma_start(T.wqs[:], T.ws[:]), [V("wqs")], [])
+    iota(V("lanes"), [[1, C]], 0, 0)
+    iota(V("table", 0, 2 * C), [[1, 2 * C]], 0, 0)
+    iota(V("table", 2 * C, 2 * C + 16), [[0, 16]], -1, 0)
+    quant("uraw", V("ut"))
     op("v", lambda: g.vector.tensor_copy(T.uqc[:].bitcast(dt.uint32), T.urawc[:].bitcast(dt.uint32).indirect(T.uoff[:, 0:8])),
        [V("uqc")], [V("urawc"), V("uoff", 0, 8)])
-    op("v", lambda: g.vector.tensor_copy(T.uqs[:], T.uraws[:].indirect(T.uoff[:, 0:8])), [V("uqs")], [V("uraws"), V("uoff", 0, 8)])
-    ts(V("c2", 0, 16), V("jj"), float(C), None, OP.add)
-    ts(V("c2", 16, 32), V("jj"), float(C), None, OP.add)
-    ts(V("i2c"), V("jj"), 2.0, 2.0 * OFF - 1, OP.mult, OP.add)
-    ts(V("cv"), V("jj"), col(6), None, OP.subtract)
-    quant("q0", V("h0"))
+    move("a", V("uqs"), (V("uraws"), V("uoff", 0, 8)))
+    quant("q0", h0)
     mm("psy", 1, "uq", 0, "q1_0")
     mm("psy", 2, "uq", 0, "q0")
     move("a", V("p1s"), P("psy", 1, C))
     move("a", V("p0s"), P("psy", 2, C))
-    for k in range(2):
-        ts(V("k16", C * k, C * k + C), V("km"), col(0), 16384.0, OP.is_equal, OP.mult)
-    ts(V("k4a"), V("km4"), col(1), 4096.0, OP.is_equal, OP.mult)
-    fill(V("xx"), float(C))
-    ts(V("k16g"), V("k16", 0, A), -512.0, None, OP.add)
-    ts(V("k4"), V("k4a"), -512.0, None, OP.add)
-    cp(V("lanes"), V("table", 0, C))
-    fill(V("table", 2 * C, 2 * C + 16), -1.0)
-    fill(V("g1", 4 * C, 4 * C + 16), 0.0)
-    for t in range(R):
-        fill(V("m0_%d" % t, 4 * C, 4 * C + 16), 0.0)
-    for a in range(4):
-        fill(V("w1", PL * a + A + C, PL * a + PL), 0.0)
 
     def logs(t):
         n = A if t else C
-        s0 = P("psx", 0, C)
+        at0 = ("psx", 0) if t else ("psy", 2)
+        s0 = P(at0[0], at0[1], C)
         m0 = V("m0_%d" % t, 0, 4 * C)
-        arrive([V("l1_%dc" % t), V("l1_%ds" % t)], 3 * t, 2 + (split if t == 0 else 0))
+        arrive([V("l1_%dc" % t), V("l1_%ds" % t)], 3 * t, 3 if t == 0 else 2)
         arrive([V("l2_%dc" % t), V("l2_%ds" % t)], 3 * t + 1, 2)
         if t:
             arrive([V("li_%d" % t)], 3 * t + 2, 1)
@@ -281,9 +286,25 @@ def rank_program(g, core, T, topo):
             lv, lo, hi = k // 2, D * (k % 2), D * (k % 2) + D
             tt(V("ff", 16 + C * lv + lo, 16 + C * lv + hi), P("psy", k % 2, D), V("mx1" if lv else "thr0", lo, hi), OP.is_gt if lv else OP.is_le)
 
+        def whole():
+            quant("gq1", V("g1", 0, 4 * C))
+            mm("psy", 0, "uq", 0, "gq1")
+
+        def late2(lv):
+            tt(V("ff", 16 + C * lv, 16 + C * lv + C), P("psy", 0, C), V("mx1" if lv else "thr0"), OP.is_gt if lv else OP.is_le)
+
         def update(q, k):
             b, h = k % 4, k // 4
             move(q, V("g1", 2 * C * h + b, 2 * C * h + 2 * C, 4), (V("w2", PL * b, PL * b + A + C), V("li_%d" % t, 16 + 8 * h, 24 + 8 * h)))
+
+        def update2(q, b):
+            move(q, V("g1", b, 4 * C, 4), (V("w2", PL * b, PL * b + A + C), V("li_%d" % t, 16, 32)))
+
+        def cap(q, _k):
+            if q == "v":
+                ts(V("kk"), V("l0"), -0.5, 2.0 ** 91, OP.add, OP.mult)
+            else:
+                act(V("kk"), V("l0"), AF.Identity, 2.0 ** 91, -2.0 ** 90)
 
         return {
             "a": lambda b: mm("psx", b, "eq", 128 * b, "l1_%d" % t),
@@ -293,17 +314,19 @@ def rank_program(g, core, T, topo):
             "m": lambda b: tt(V("m0_0", b, 4 * C, 4), P("psx", b, C), V("h0", b, 4 * C, 4), OP.add),
             "ma": lambda: dma("g", lambda: g.dma_start(ap(m0), ap(G0(t)), accum_op=OP.add), [m0], [G0(t), m0]),
             "q0": lambda: quant("gq0", G0(t)),
-            "s0": lambda: mm("psx", 0, "uq", 0, "gq0"),
+            "s0": lambda: mm(at0[0], at0[1], "uq", 0, "gq0"),
             "d": lambda b: mm("psy", b, "eq", 128 * b, "l2_%d" % t),
             "f": lambda q, b: move(q, V("w2", PL * b, PL * b + A) if t else V("g1", b, 4 * C, 4), P("psy", b, n)),
-            "u": update, "p": score1, "l": late,
+            "u": update, "p": score1, "l": late, "pp": whole, "L": late2, "U": update2,
             "c0": lambda: tt(V("l0"), s0, V("p0s"), OP.is_gt),
             "c1": lambda: tt(V("mx1"), s0, V("p1s"), OP.max),
-            "k": lambda q, _k: ts(V("kk"), V("l0"), -0.5, 2.0 ** 91, OP.add, OP.mult),
+            "k": cap,
             "c3": lambda: tt(V("thr0"), s0, V("kk"), OP.min),
         }
 
     def replay(t):
+        gv = PLAN["g1v"]
+
         def replay1():
             quant("zq1", V("z1"))
             for a in range(4):
@@ -325,20 +348,16 @@ def rank_program(g, core, T, topo):
             ts(V("u1", 0, 9), V("u2", 0, 9), 0.5, col(5), OP.mult, OP.add)
             tt(V("s2", 0, 9), V("h16", 15, A, 16), V("u1", 0, 9), OP.add)
 
-        def where0():
-            if t:
-                tt(V("mn"), V("aa", 0, 16), V("aa", 16, 32), OP.min)
-
         def where1():
             if t:
-                tt(V("ix"), V("mn"), V("iy"), OP.min)
+                tt(V("ix"), V("mn", 16, 32), V("iy"), OP.min)
 
         def where2():
             if t < R - 1:
-                ts(V("iy"), V("ix" if t else "mb"), float(A), None, OP.add)
+                ts(V("iy"), V("ix") if t else V("ma", 16, 32), float(A), None, OP.add)
             else:
                 for a in range(4):
-                    ts(V("l4", 16 * a, 16 * a + 16), V("ix"), 4.0, a - 4.0 * OFF, OP.mult, OP.add)
+                    ts(V("l4", 16 * a, 16 * a + 16), V("ix"), 4.0, float(a), OP.mult, OP.add)
 
         def once():
             if t == 0:
@@ -351,10 +370,29 @@ def rank_program(g, core, T, topo):
             move("v", V("ysb"), P("psx", 0, C))
             dma("s", lambda: g.sync.dma_start(T.y[:], T.ysb[:]), [], [V("ysb")])
 
+        def gather_half(q, k):
+            a, h = k % 4, k // 4
+            move(q, V("h2", 2 * C * h + a, 2 * C * h + 2 * C, 4), (V("hw"), V("l4", 16 * a + 8 * h, 16 * a + 8 * h + 8)))
+
+        def pack_half(h):
+            quant("q2_3", V("h2", 2 * C * h, 2 * C * h + 2 * C), D * h, D * h + D)
+            mm("psx", h, "vq", 0, "q2_3", D * h, D * h + D)
+            dma("s", lambda: g.sync.dma_start(T.oc[:, 4 * D * h:4 * D * h + 4 * D], T.q2_3c[:, D * h:D * h + D].bitcast(dt.uint8)), [],
+                [V("q2_3c", D * h, D * h + D)])
+
+        def store_half(q, h):
+            move(q, V("ysb", D * h, D * h + D), P("psx", h, D))
+            dma("s", lambda: g.sync.dma_start(T.y[:, D * h:D * h + D], T.ysb[:, D * h:D * h + D]), [], [V("ysb", D * h, D * h + D)])
+
         return {
             "r": lambda q, a: relu(q, V("w1", PL * a, PL * a + A), P("psx", a, A), 2.0 ** -6),
             "z": lambda a: tt(V("z1", a, 4 * A, 4), (V("w1", PL * a, PL * a + PL), V("list2", 0, 9)), V("g1e", a, 4 * A, 4), OP.add),
             "n": lambda q, a: move(q, V("t0", a, 4 * A, 4), V("w1", PL * a, PL * a + A), 2.0),
+            "R": lambda q, a: relu(q, V("t0", a, 4 * A, 4), P("psx", a, A), 2.0 ** -5),
+            "N": lambda q, a: move(q, V("w1", PL * a, PL * a + A), V("t0", a, 4 * A, 4), 0.5),
+            "gv": lambda: move("v", V("g1e", 0, 16 * gv), (V("g1"), V("e4", 0, gv)), 0.5) if gv else None,
+            "ga": lambda: move("a", V("g1e", 16 * gv, 4 * A), (V("g1"), V("e4", gv)), 0.5),
+            "j2": lambda: ts(V("list2", 0, 9), V("s1", 0, 9), col(6), None, OP.add),
             "qz": replay1,
             "h": lambda q, a: move(q, V("h1_%d" % (t + 1), a, 4 * C, 4), (V("w1", PL * a, PL * a + A + C), V("il_%d" % t, 0, 16)), 2.0),
             "t": lambda q, a: relu(q, T1(t, a, 4), P("psy", a, A), 2.0 ** -5),
@@ -362,58 +400,65 @@ def rank_program(g, core, T, topo):
             "P": lambda q, _k: move(q, V("p1s"), P("psy", 3, C)),
             "K0": keys, "K1": lambda: cp(V("cl", 0, 9), V("s2", 0, 9)),
             "K2": lambda: move("a", V("olr", A * t, A * t + A), (V("table"), V("cl", 0, 9))),
-            "W0": where0, "W1": where1, "W2": where2, "vq": once,
+            "W1": where1, "W2": where2, "vq": once,
             "G": lambda q, a: move(q, V("h2", a, 4 * C, 4), (V("hw"), V("l4", 16 * a, 16 * a + 16))),
-            "xx": outputs,
+            "xx": outputs, "g": gather_half, "x": pack_half, "y": store_half,
         }
 
-    play(PLAN["rx0"], logs(0))
-    for t in range(R):
-        last = t == R - 1
-        for a in range(4):
-            move("a", V("w1", PL * a + A, PL * a + A + C), V("h1_%d" % t, a, 4 * C, 4), 0.5)
-        if not last:
-            for a in range(4):
-                move("a", V("w2", PL * a + A, PL * a + A + C), V("g1", a, 4 * C, 4))
-            dma("s", lambda t=t: g.sync.dma_start(T["m0_%d" % (t + 1)][:, 0:4 * C], T.x[:, 0:4 * C]), [V("m0_%d" % (t + 1), 0, 4 * C)],
-                [V("m0_%d" % t, 0, 4 * C)])
-        if t == 0:
-            dma("s", lambda: g.sync.dma_start(T.vt[:], T.v[:]), [V("vt")], [])
-        i2 = V("il_%d" % t, 16, 32)
-        scan(V("yy"), V("ff", 15, 15 + 2 * C), V("ff", 16, 16 + 2 * C), 2.0 * OFF - 1, OP.add, OP.add)
-        scan(V("hd"), V("k16"), V("yy"), 0.0, OP.add, OP.min)
-        cp(V("y255", 0, 1), V("yy", C - 1, C))
-        ts(V("wi"), V("hd", 15, 2 * C, 16), 2049.0, None, OP.mult)
-        ts(V("u2", 0, 9), V("i2c", 0, 9), V("y255", 0, 1), 512.0, OP.is_ge, OP.mult)
-        ts(V("aa"), V("wi"), 1, 255 + 1024 + 2 ** 19, OP.arith_shift_right, OP.bitwise_and)
-        tt(V("vv", 0, 9), V("u2", 0, 9), V("cv", 0, 9), OP.add)
-        tt(V("ma"), V("aa"), V("c2"), OP.min)
-        tt(V("mb"), V("ma", 0, 16), V("ma", 16, 32), OP.min)
-        if not last:
-            ts(V("il_%d" % t, 0, 16), V("ma", 0, 16), -float(OFF), None, OP.add)
-        ts(i2, V("mb"), -float(OFF), None, OP.add)
-        if not last:
-            remote(V("il_%d" % t), V("li_%d" % (t + 1)), 3 * t + 5, "sent1")
-        xw, xs = V("xx", XW * t, XW * t + XW), V("xx", XW * t, XW * t + A)
-        cp((xw, i2), V("lanes"))
-        scan(V("h4"), V("k4"), xs, 0.0, OP.add, OP.min)
-        scan(V("h16"), V("k16g"), xs, 0.0, OP.add, OP.min)
-        ts(V("e4"), V("h4", 3, A, 4), 4.0, col(4), OP.mult, OP.add)
-        zv, gv = PLAN["z0v"], PLAN["g1v"]
-        move("a", V("z0", 16 * zv, 4 * A), (V("m0_%d" % t), V("e4", zv)), 0.5)
-        move("v", V("z0", 0, 16 * zv), (V("m0_%d" % t), V("e4", 0, zv)), 0.5)
-        tt(V("s1", 0, 9), V("h16", 15, A, 16), V("vv", 0, 9), OP.min)
-        quant("zq0", V("z0"))
-        for a in range(4):
-            mm("psx", a, "wq", 128 * a, "zq0")
-        move("a", V("g1e", 16 * gv, 4 * A), (V("g1"), V("e4", gv)), 0.5)
-        ts(V("list2", 0, 9), V("s1", 0, 9), col(6), None, OP.add)
-        move("v", V("g1e", 0, 16 * gv), (V("g1"), V("e4", 0, gv)), 0.5)
-        calls = replay(t)
-        if not last:
-            calls.update(logs(t + 1))
-        play(PLAN["end" if last else "mid"], calls)
+    def lists(t):
+        i2, xw, xs = V("i2"), V("xx", XW * t, XW * t + XW), V("xx", XW * t, XW * t + A)
+        zv = PLAN["z0v"]
 
+        def loads():
+            dma("s", lambda: g.sync.dma_start(T["m0_%d" % (t + 1)][:, 0:4 * C], T.x[:, 0:4 * C]), [V("m0_%d" % (t + 1), 0, 4 * C)],
+                [V("m0_%d" % t, 0, 4 * C)])
+            if t == 0:
+                dma("s", lambda: g.sync.dma_start(T.vt[:], T.v[:]), [V("vt")], [])
+
+        def replay0():
+            quant("zq0", V("z0"))
+            for a in range(4):
+                mm("psx", a, "wq", 128 * a, "zq0")
+
+        return {
+            "O": lambda q, a: move(q, V("w1", PL * a + A, PL * a + A + C), V("h1_%d" % t, a, 4 * C, 4), 0.5),
+            "B": lambda q, a: move(q, V("w2", PL * a + A, PL * a + A + C), V("g1", a, 4 * C, 4)),
+            "sy": lambda: scan(V("yy"), V("ff", 15, 15 + 2 * C), V("ff", 15, 15 + 2 * C), 0.0, OP.add, OP.max),
+            "sh": lambda: scan(V("hd"), V("k16"), V("yy"), 0.0, OP.add, OP.min),
+            "F": lambda lv: scan(V("hf", C * lv, C * lv + C), V("ff", 16 + C * lv, 16 + C * lv + C), V("kf", 0, C), 0.0, OP.max, OP.mult),
+            "hf": lambda: scan(V("hf"), V("ff", 16, 16 + 2 * C), V("kf"), 0.0, OP.max, OP.mult),
+            "pr": lambda: tt(V("pre"), V("hf", 15, 2 * C, 16), V("cn"), OP.add),
+            "aa": lambda: tt(V("aa"), V("hd", 15, 2 * C, 16), V("pre"), OP.max),
+            "mb": lambda: tt(V("aa", 16, 32), V("aa", 0, 16), V("aa", 16, 32), OP.min),
+            "i2": lambda: ts(i2, V("aa", 16, 32), 0.25, None, OP.add),
+            "b0": lambda: ts(V("ab"), V("aa"), 0.5 - A, 4096.0, OP.add, OP.mult),
+            "b1": lambda: tt(V("mn"), V("aa"), V("ab"), OP.max),
+            "b2": lambda: tt(V("ma"), V("mn"), V("c2"), OP.min),
+            "i0": lambda: cp(V("il_%d" % t), V("ma")),
+            "u2": lambda: ts(V("u2", 0, 9), V("jj", 0, 9), V("yy", C, C + 1), 512.0, OP.is_ge, OP.mult),
+            "vv": lambda: tt(V("vv", 0, 9), V("u2", 0, 9), V("cv", 0, 9), OP.add),
+            "ls": lambda: remote(V("il_%d" % t), V("li_%d" % (t + 1)), 3 * t + 5, "sent1"),
+            "sc": lambda: cp((xw, i2), V("lanes")),
+            "ld": loads,
+            "M": lambda b: tt(V("m0_0", b, 4 * C, 4), P("psx", b, C), V("h0", b, 4 * C, 4), OP.add) if t == 0 and not PLAN["acc0"] else None,
+            "h4": lambda: scan(V("h4"), V("k4"), xs, 0.0, OP.add, OP.min),
+            "h6": lambda: scan(V("h16"), V("k16g"), xs, 0.0, OP.add, OP.min),
+            "e4": lambda: ts(V("e4"), V("h4", 3, A, 4), 4.0, col(4), OP.mult, OP.add),
+            "Za": lambda: move("a", V("z0", 16 * zv, 4 * A), (V("m0_%d" % t), V("e4", zv)), 0.5),
+            "Zv": lambda: move("v", V("z0", 0, 16 * zv), (V("m0_%d" % t), V("e4", 0, zv)), 0.5),
+            "s1": lambda: tt(V("s1", 0, 9), V("h16", 15, A, 16), V("vv", 0, 9), OP.min),
+            "qy": replay0,
+        }
+
+    play(PLAN["rx0"], logs(0), "s")
+    for t in range(R):
+        calls = lists(t)
+        calls.update(replay(t))
+        if t < R - 1:
+            calls.update(logs(t + 1))
+        play(PLAN["mid" if t < R - 1 else "end"], calls, t)
+
+    TAG[0] = "z"
     dma("a", lambda: g.scalar.dma_start(T.ol[:], T.olr[0:128:16, :]), [], [V("olr")])
     for k in range(4):
         dma("a", lambda k=k: g.scalar.dma_start(T.osc[4 * k:4 * k + 4, :], T.q2_3s[32 * k:32 * k + 4, :]), [], [V("q2_3s")])

@@ -21,7 +21,7 @@ def _pairs(names, n):
 
 
 _bufs("h0 h1_0 h1_1 h1_2 h2", 4 * C, BF)
-_bufs("gw_0 gw_1 gw_2", 4 * A + 4 * C, BF)
+_bufs("g0", 4 * C, BF)
 _bufs("hw", R * 4 * A + 4 * C, BF)
 _bufs("g1 m0_0 m0_1 m0_2", 4 * C + 16, BF)
 _bufs("ut vt", 512, BF)
@@ -31,35 +31,37 @@ _bufs("et", 516, BF)
 _pairs("q0 q1_0 qh q2_0 q2_3 l1_0 l2_0 gq0 gq1", C)
 _pairs("zq0 zq1 q1_1 q1_2 l1_1 l1_2 q2_1 q2_2 l2_1 l2_2", A)
 _bufs("p0s p1s mx1 thr0 ysb", C, F32)
-_bufs("l0 kk lanes km", C, BF)
+_bufs("lanes km", C, BF)
 _bufs("ff", 2 * C + 16, F16)
 _bufs("yy hd hf k16 kf", 2 * C, BF)
-_bufs("k16g k4 k4a h4", A, F16)
-_bufs("km4", A, BF)
+_bufs("h4", A, F16)
+_bufs("km4 k16g k4 k4a", A, BF)
 _bufs("kg", C, BF)
-_bufs("h16", A, F32)
+_bufs("h16", R * A, F32)
+_bufs("u1 s2", 32, F32)
+_bufs("cl", 32, U16)
 _bufs("pre aa ab mn ma c2 cn", 32, F32)
 _bufs("ix iy", 16, F32)
 _bufs("pi", 16, I32)
-_bufs("list2 cl uoff i2", 16, U16)
+_bufs("list2 uoff i2", 16, U16)
 _bufs("e4", A // 4, U16)
-_bufs("l4 lb", 64, U16)
+_bufs("l4", 64, U16)
 _bufs("il_0 il_1 li_1 li_2", 32, U16)
-_bufs("col jq jj cv u1 u2 vv s1 s2", 16, F32)
+_bufs("col jq jj cv u2 vv s1", 16, F32)
 _bufs("xx", R * XW, BF)
 _bufs("table", 2 * C + 16, F32)
 _bufs("idv", 128, F32)
-_bufs("w1 w2", 4 * PL, BF)
+_bufs("w0 w1 w2", 4 * PL, BF)
 _bufs("z0 z1 g1e t0", 4 * A, BF)
 _bufs("olr", R * A, F32)
 
-SEMAPHORES = ["cv", "ca", "cp", "cg", "sent0", "sent1"] + ["arr%d" % k for k in range(3 * R)] + ["d%d" % k for k in range(30)]
+SEMAPHORES = ["cv", "ca", "cp", "cg", "sent0", "sent1", "sent2", "go"] + ["arr%d" % k for k in range(3 * R)] + ["d%d" % k for k in range(30)]
 
 PLAN = {
-    "acc0": 0, "z0v": 18, "g1v": 10,
-    "rx0": "a1 a3 a2 a0 d2 d3 ev1 ea3 ev0 d1 ea2 d0 q0 fa2 fa3 fv1 s0 fa0 c0 p0 p1 c1 ka0 c3 l3 l2 l0 l1",
-    "mid": "M0 sy Oa0 hf sh Oa1 pr M2 aa M3 mb M1 i2 Oa2 Oa3 u2 sc Ba0 Ba3 b0 ld h4 Ba2 h6 e4 b1 Zv vv Ba1 b2 Za qy s1 gv j2 ga rv0 i0 ra1 rv2 ra3 ls nv0 na2 z0 nv3 na1 ha3 z3 o1 z1 ha1 ha2 z2 W1 qz K0 ta0 ta2 tv1 ha0 a0 tv3 a1 a3 o2 ea0 ea1 lb a2 ea2 qh ev3 wv1 d2 wa3 wa2 d1 d0 Pa0 wv0 d3 fa2 W2 vq q0 s0 ma fv1 uv2 fa0 fa3 uv1 uv0 ua5 ua3 ua4 c0 p0 ua7 uv6 c1 p1 ka0 c3 l2 l0 l3 l1 K1 K2",
-    "end": "sy hf Oa1 sh pr u2 Oa0 aa vv mb Oa2 Oa3 i2 sc b0 h4 h6 e4 s1 Zv Za ga j2 b1 qy gv ra0 K0 ra1 z0 z1 ra2 z2 ra3 z3 W1 qz W2 ta0 ta2 tv1 tv3 gv6 ga7 gv5 ga4 x1 ga3 gv1 ga2 gv0 K1 ya1 x0 K2 yv0",
+    "h0w": 3, "acc0": 0, "z0v": 18, "g1v": 6,
+    "rx0": "Q0 a3 a1 ev3 A0 S0 a0 a2 d1 ea1 ev2 ea0 q0 fa1 d2 d3 d0 fa2 fv3 s0 Q1 fa0 p0 A1 p1 c1 S1 T0 l0 T1 l1 J0 J1",
+    "mid": "E0 E1 E2 E3 tb Oa0 Oa1 F1 sy F0 pb sh pa M0 aa Oa2 Oa3 u2 mb Ba0 Xa0 M2 i2 M3 Xa1 Ba1 Ba2 Ba3 sc M1 ld h4 e4 b1 Zv h6 Za ga vv qy gv b2 s1 i0 j2 rv1 ra0 rv2 ra3 z0 na0 z1 ls na1 na3 z3 na2 z2 o1 qz hv2 W1 ha1 a1 tv1 ha3 a3 ta0 ta2 tv3 a0 a2 ha0 o2 ea1 qh ea2 ev3 d2 Xa2 ev0 wa3 wv1 d0 Pv0 wv0 wa2 fa2 fv0 q0 ma d1 fa1 d3 fa3 uv0 ua2 uv1 uv5 s0 ua4 ua3 uv6 ua7 p0 p1 c1 T0 l0 T1 J0 l1 J1",
+    "end": "F1 sy F0 Oa0 Oa1 Oa2 Oa3 pb pa sh u2 vq aa vv mb i2 Xa0 sc h4 e4 Zv Za h6 Xa1 b1 qy gv s1 W1 K0 j2 rv0 K1 ga ra2 rv1 z0 ra3 z1 K2 z3 z2 W2 qz ta0 tv1 K3 ta2 tv3 gv5 ga4 ga7 ga2 gv6 gv1 ga0 gv3 x1 x0 ya1 ya0",
 }
 
 
@@ -77,7 +79,7 @@ def rank_program(g, core, T, topo):
     ops = []
     TAG = [None]
     PLAN["ops"] = ops
-    sent = {"sent0": 0, "sent1": 0}
+    sent = {"sent0": 0, "sent1": 0, "sent2": 0}
 
     def V(name, a=0, b=None, s=1):
         return (name, a, SCRATCH[name][1][1] if b is None else b, s)
@@ -124,8 +126,16 @@ def rank_program(g, core, T, topo):
         kw = {k: ap(x) for k, x, plain in (("scale", scale, 1.0), ("bias", bias, 0.0)) if x != plain}
         op("a", lambda: g.scalar.activation(ap(o), ap(i), f, **kw), [o], [i, bias])
 
-    def move(q, o, i, scale=1.0):
+    def affine(q, o, i, scale, bias):
         if q == "a":
+            act(o, i, AF.Identity, scale, bias)
+        else:
+            ts(o, i, scale, bias, OP.mult, OP.add)
+
+    def move(q, o, i, scale=1.0):
+        if q == "g":
+            op("g", lambda: g.affine_select(ap(o), ap(i), [[0, o[2] - o[1]]], OP.is_gt, 0.0, 1, 0), [o], [i])
+        elif q == "a":
             act(o, i, AF.Copy, scale)
         elif scale == 1.0:
             cp(o, i)
@@ -175,7 +185,7 @@ def rank_program(g, core, T, topo):
         return V("col", k, k + 1)
 
     def G0(t, a=0, s=1):
-        return V("gw_%d" % t, 4 * A + a, 4 * A + 4 * C, s)
+        return V("g0", a, 4 * C, s)
 
     def T1(t, a=0, s=1):
         return V("hw", 4 * A * (R - 1 - t) + a, 4 * A * (R - t), s)
@@ -196,7 +206,10 @@ def rank_program(g, core, T, topo):
     dma("s", lambda: g.sync.dma_start(T.h1_0[:, 2 * C:4 * C], T.x[:, 6 * C:8 * C]), [V("h1_0", 2 * C, 4 * C)], [])
     dma("s", lambda: g.sync.dma_start(ap(h2x), T.x[:, 8 * C:12 * C]), [h2x], [])
     dma("s", lambda: g.sync.dma_start(T.ut[:], T.u[:]), [V("ut")], [])
-    dma("s", lambda: g.sync.dma_start(ap(h0), T.x[:, 0:4 * C]), [h0], [])
+    h0a, h0b = V(h0[0], 0, 2 * C), V(h0[0], 2 * C, 4 * C)
+    dma("s", lambda: g.sync.dma_start(ap(h0a), T.x[:, 0:2 * C]), [h0a], [])
+    if not PLAN["h0w"]:
+        dma("s", lambda: g.sync.dma_start(ap(h0b), T.x[:, 2 * C:4 * C]), [h0b], [])
 
     def const(o, c):
         act(o, V("et", 0, o[2] - o[1]), AF.Identity, 0.0, c)
@@ -216,53 +229,58 @@ def rank_program(g, core, T, topo):
         quant("eq", V("et", 3 - b, 515 - b), 128 * b, 128 * b + 128)
     cp(V("col", 0, 3), V("pi", 1, 4))
     cp(V("uoff", 0, 8), V("jq", 0, 8))
-    ts(col(3), col(1), -2048.0, 6144.0, OP.mult, OP.add)
-    ts(col(5), col(0), -512.0, 7680.0, OP.mult, OP.add)
-    ts(V("jj"), V("jq"), col(0), None, OP.add)
     for t in range(R):
         const(V("xx", XW * t, XW * t + A), float(C))
         const(V("m0_%d" % t, 4 * C, 4 * C + 16), 0.0)
     const(V("g1", 4 * C, 4 * C + 16), 0.0)
     for a in range(4):
         const(V("w1", PL * a + A + C, PL * a + PL), 0.0)
+    const(V("cn", 0, 16), 2.0 * XW)
+    affine("a", col(3), col(1), -2048.0, 6144.0)
+    affine("a", col(5), col(0), -512.0, 7680.0)
+    affine("a", col(6), col(0), -512.0, 7680.0 + A)
+    affine("a", col(7), col(0), 513.0, -7680.0 - A)
+    affine("a", V("jj"), V("jq"), 1.0, col(0))
+    affine("a", col(4), col(3), 1.0, col(2))
+    affine("a", V("cv"), V("jq"), 1.0, col(7))
+    for k in range(2):
+        affine("a", V("c2", 16 * k, 16 * k + 16), V("jj"), 1.0, float(A))
+    affine("a", V("cn", 16, 32), V("jj"), 1.0, XW - C - 8.0)
 
     quant("q1_0", V("h1_0", 0, 2 * C), 0, D)
     remote(V("q1_0c", 0, D), V("l1_0c", 0, D), 0, "sent0")
-    tt(col(4), col(3), col(2), OP.add)
-    ts(col(6), col(5), float(A), None, OP.add)
-    for k in range(2):
-        act(V("c2", 16 * k, 16 * k + 16), V("jj"), AF.Identity, 1.0, float(A))
-    const(V("cn", 0, 16), 2.0 * XW)
-    act(V("cn", 16, 32), V("jj"), AF.Identity, 1.0, XW - C - 8.0)
     ts(V("kg"), V("km"), col(0), None, OP.is_gt)
+    ts(V("k16", 0, C), V("km"), col(0), 16384.0, OP.is_equal, OP.mult)
     quant("q1_0", V("h1_0", 2 * C, 4 * C), D, C)
     remote(V("q1_0c", D, C), V("l1_0c", D, C), 0, "sent0")
     remote(V("q1_0s"), V("l1_0s"), 0, "sent0")
-    ts(V("k16", 0, C), V("km"), col(0), 16384.0, OP.is_equal, OP.mult)
-    ts(V("cv"), V("jj"), col(6), None, OP.subtract)
     ts(V("k4a"), V("km4"), col(1), 4096.0, OP.is_equal, OP.mult)
     tt(V("kf", 0, C), V("kg"), V("k16", 0, C), OP.add)
     move("a", V("k16", C, 2 * C), V("k16", 0, C))
+    affine("a", V("k16g"), V("k16", 0, A), 1.0, -512.0)
+    affine("a", V("k4"), V("k4a"), 1.0, -512.0)
     move("a", V("kf", 15, C, 16), V("kf", 15, C, 16), -0.25)
     move("a", V("kf", C, 2 * C), V("kf", 0, C))
-    ts(V("k16g"), V("k16", 0, A), -512.0, None, OP.add)
-    ts(V("k4"), V("k4a"), -512.0, None, OP.add)
     quant("q2_0", h2x)
-    send("q2_0", "l2_0", 1, "sent0")
-    dma("s", lambda: g.sync.dma_start(T.wqc[:].bitcast(dt.uint8), T.wc[:]), [V("wqc")], [], pre=("sent0", 5 * n_out))
-    dma("s", lambda: g.sync.dma_start(T.wqs[:], T.ws[:]), [V("wqs")], [])
+    send("q2_0", "l2_0", 1, "sent2")
+    if PLAN["h0w"] == 3:
+        op("g", lambda: g.sem_inc(T.sem.go, 1), [], [])
+        dma("s", lambda: g.sync.dma_start(ap(h0b), T.x[:, 2 * C:4 * C]), [h0b], [], pre=("go", 1))
+    elif PLAN["h0w"]:
+        dma("s", lambda: g.sync.dma_start(ap(h0b), T.x[:, 2 * C:4 * C]), [h0b], [V("q2_0s")] if PLAN["h0w"] == 2 else [],
+            pre=("sent0", 3 * n_out) if PLAN["h0w"] == 1 else None)
+    dma("s", lambda: g.sync.dma_start(T.wqc[:].bitcast(dt.uint8), T.wc[:]), [V("wqc")], [], pre=("sent2", 2 * n_out))
+    if PLAN["acc0"]:
+        dma("g", lambda: g.dma_start(T.wqs[:], T.ws[:]), [V("wqs")], [])
+    else:
+        dma("s", lambda: g.sync.dma_start(T.wqs[:], T.ws[:]), [V("wqs")], [])
     iota(V("lanes"), [[1, C]], 0, 0)
-    iota(V("table", 0, 2 * C), [[1, 2 * C]], 0, 0)
-    iota(V("table", 2 * C, 2 * C + 16), [[0, 16]], -1, 0)
     quant("uraw", V("ut"))
     op("v", lambda: g.vector.tensor_copy(T.uqc[:].bitcast(dt.uint32), T.urawc[:].bitcast(dt.uint32).indirect(T.uoff[:, 0:8])),
        [V("uqc")], [V("urawc"), V("uoff", 0, 8)])
     move("a", V("uqs"), (V("uraws"), V("uoff", 0, 8)))
-    quant("q0", h0)
     mm("psy", 1, "uq", 0, "q1_0")
-    mm("psy", 2, "uq", 0, "q0")
     move("a", V("p1s"), P("psy", 1, C))
-    move("a", V("p0s"), P("psy", 2, C))
 
     def logs(t):
         n = A if t else C
@@ -274,24 +292,26 @@ def rank_program(g, core, T, topo):
         if t:
             arrive([V("li_%d" % t)], 3 * t + 2, 1)
 
-        def lists_b():
-            for b in range(4):
-                ts(V("lb", 16 * b, 16 * b + 16), V("li_%d" % t, 0, 16), 4.0, float(b), OP.mult, OP.add)
-
         def score1(h):
             quant("gq1", V("g1", 2 * C * h, 2 * C * h + 2 * C), D * h, D * h + D)
             mm("psy", h, "uq", 0, "gq1", D * h, D * h + D)
 
         def late(k):
-            lv, lo, hi = k // 2, D * (k % 2), D * (k % 2) + D
-            tt(V("ff", 16 + C * lv + lo, 16 + C * lv + hi), P("psy", k % 2, D), V("mx1" if lv else "thr0", lo, hi), OP.is_gt if lv else OP.is_le)
+            tt(V("ff", 16 + C + D * k, 16 + C + D * k + D), P("psy", k, D), V("mx1", D * k, D * k + D), OP.is_gt)
 
         def whole():
             quant("gq1", V("g1", 0, 4 * C))
             mm("psy", 0, "uq", 0, "gq1")
 
         def late2(lv):
-            tt(V("ff", 16 + C * lv, 16 + C * lv + C), P("psy", 0, C), V("mx1" if lv else "thr0"), OP.is_gt if lv else OP.is_le)
+            if lv:
+                tt(V("ff", 16 + C, 16 + 2 * C), P("psy", 0, C), V("mx1"), OP.is_gt)
+            else:
+                tt(V("ff", 16, 16 + C), s0, V("thr0"), OP.is_ge)
+
+        def own0(h):
+            quant("q0", V(h0[0], 2 * C * h, 2 * C * h + 2 * C), D * h, D * h + D)
+            mm("psy", 3, "uq", 0, "q0", D * h, D * h + D)
 
         def update(q, k):
             b, h = k % 4, k // 4
@@ -308,9 +328,8 @@ def rank_program(g, core, T, topo):
 
         return {
             "a": lambda b: mm("psx", b, "eq", 128 * b, "l1_%d" % t),
-            "e": lambda q, b: move(q, V("gw_%d" % (t - 1), b, 4 * A, 4) if t else G0(t, b, 4), P("psx", b, n)),
-            "lb": lists_b,
-            "w": lambda q, b: move(q, G0(t, b, 4), (V("gw_%d" % (t - 1)), V("lb", 16 * b, 16 * b + 16))),
+            "e": lambda q, b: move(q, V("w0", PL * b, PL * b + A) if t else G0(t, b, 4), P("psx", b, n)),
+            "w": lambda q, b: move(q, G0(t, b, 4), (V("w0", PL * b, PL * b + A + C), V("li_%d" % t, 0, 16))),
             "m": lambda b: tt(V("m0_0", b, 4 * C, 4), P("psx", b, C), V("h0", b, 4 * C, 4), OP.add),
             "ma": lambda: dma("g", lambda: g.dma_start(ap(m0), ap(G0(t)), accum_op=OP.add), [m0], [G0(t), m0]),
             "q0": lambda: quant("gq0", G0(t)),
@@ -318,7 +337,11 @@ def rank_program(g, core, T, topo):
             "d": lambda b: mm("psy", b, "eq", 128 * b, "l2_%d" % t),
             "f": lambda q, b: move(q, V("w2", PL * b, PL * b + A) if t else V("g1", b, 4 * C, 4), P("psy", b, n)),
             "u": update, "p": score1, "l": late, "pp": whole, "L": late2, "U": update2,
-            "c0": lambda: tt(V("l0"), s0, V("p0s"), OP.is_gt),
+            "T": lambda h: tt(V("thr0", D * h, D * h + D), P("psy", h, D), V("p0s", D * h, D * h + D), OP.max),
+            "TT": lambda: tt(V("thr0"), P("psy", 0, C), V("p0s"), OP.max),
+            "J": lambda h: tt(V("ff", 16 + D * h, 16 + D * h + D), V(s0[0], s0[1] + D * h, s0[1] + D * h + D), V("thr0", D * h, D * h + D), OP.is_ge),
+            "Q": own0, "A": lambda h: act(V("ysb", D * h, D * h + D), P("psy", 3, D), AF.Abs, 5 * 2.0 ** -26, 2.0 ** -124),
+            "S": lambda h: tt(V("p0s", D * h, D * h + D), P("psy", 3, D), V("ysb", D * h, D * h + D), OP.add),
             "c1": lambda: tt(V("mx1"), s0, V("p1s"), OP.max),
             "k": cap,
             "c3": lambda: tt(V("thr0"), s0, V("kk"), OP.min),
@@ -345,8 +368,7 @@ def rank_program(g, core, T, topo):
             mm("psy", 3, "uq", 0, "qh")
 
         def keys():
-            ts(V("u1", 0, 9), V("u2", 0, 9), 0.5, col(5), OP.mult, OP.add)
-            tt(V("s2", 0, 9), V("h16", 15, A, 16), V("u1", 0, 9), OP.add)
+            tt(V("s2", 0, 9 * R), V("h16", 15, R * A, 16), V("u1", 0, 9 * R), OP.add)
 
         def where1():
             if t:
@@ -360,8 +382,7 @@ def rank_program(g, core, T, topo):
                     ts(V("l4", 16 * a, 16 * a + 16), V("ix"), 4.0, float(a), OP.mult, OP.add)
 
         def once():
-            if t == 0:
-                quant("vq", V("vt"))
+            quant("vq", V("vt"))
 
         def outputs():
             quant("q2_3", V("h2"))
@@ -389,7 +410,6 @@ def rank_program(g, core, T, topo):
             "z": lambda a: tt(V("z1", a, 4 * A, 4), (V("w1", PL * a, PL * a + PL), V("list2", 0, 9)), V("g1e", a, 4 * A, 4), OP.add),
             "n": lambda q, a: move(q, V("t0", a, 4 * A, 4), V("w1", PL * a, PL * a + A), 2.0),
             "R": lambda q, a: relu(q, V("t0", a, 4 * A, 4), P("psx", a, A), 2.0 ** -5),
-            "N": lambda q, a: move(q, V("w1", PL * a, PL * a + A), V("t0", a, 4 * A, 4), 0.5),
             "gv": lambda: move("v", V("g1e", 0, 16 * gv), (V("g1"), V("e4", 0, gv)), 0.5) if gv else None,
             "ga": lambda: move("a", V("g1e", 16 * gv, 4 * A), (V("g1"), V("e4", gv)), 0.5),
             "j2": lambda: ts(V("list2", 0, 9), V("s1", 0, 9), col(6), None, OP.add),
@@ -398,8 +418,9 @@ def rank_program(g, core, T, topo):
             "t": lambda q, a: relu(q, T1(t, a, 4), P("psy", a, A), 2.0 ** -5),
             "o1": out1, "o2": out2, "qh": own1,
             "P": lambda q, _k: move(q, V("p1s"), P("psy", 3, C)),
-            "K0": keys, "K1": lambda: cp(V("cl", 0, 9), V("s2", 0, 9)),
-            "K2": lambda: move("a", V("olr", A * t, A * t + A), (V("table"), V("cl", 0, 9))),
+            "K0": keys, "K1": lambda: cp(V("cl", 0, 9 * R), V("s2", 0, 9 * R)),
+            "K2": lambda: move("a", V("olr"), (V("table"), V("cl", 0, 9 * R))),
+            "K3": lambda: dma("s", lambda: g.sync.dma_start(T.ol[:], T.olr[0:128:16, :]), [], [V("olr")]),
             "W1": where1, "W2": where2, "vq": once,
             "G": lambda q, a: move(q, V("h2", a, 4 * C, 4), (V("hw"), V("l4", 16 * a, 16 * a + 16))),
             "xx": outputs, "g": gather_half, "x": pack_half, "y": store_half,
@@ -413,7 +434,12 @@ def rank_program(g, core, T, topo):
             dma("s", lambda: g.sync.dma_start(T["m0_%d" % (t + 1)][:, 0:4 * C], T.x[:, 0:4 * C]), [V("m0_%d" % (t + 1), 0, 4 * C)],
                 [V("m0_%d" % t, 0, 4 * C)])
             if t == 0:
-                dma("s", lambda: g.sync.dma_start(T.vt[:], T.v[:]), [V("vt")], [])
+                dma("g", lambda: g.dma_start(T.vt[:], T.v[:]), [V("vt")], [])
+
+        def table():
+            if t == 0:
+                iota(V("table", 0, 2 * C), [[1, 2 * C]], 0, 0)
+                iota(V("table", 2 * C, 2 * C + 16), [[0, 16]], -1, 0)
 
         def replay0():
             quant("zq0", V("z0"))
@@ -423,10 +449,19 @@ def rank_program(g, core, T, topo):
         return {
             "O": lambda q, a: move(q, V("w1", PL * a + A, PL * a + A + C), V("h1_%d" % t, a, 4 * C, 4), 0.5),
             "B": lambda q, a: move(q, V("w2", PL * a + A, PL * a + A + C), V("g1", a, 4 * C, 4)),
+            "C": lambda q, a: move(q, V("w0", PL * a + A, PL * a + A + C), V("g0", a, 4 * C, 4)),
+            "D": lambda a: move("g", V("w2", PL * a + A, PL * a + A + C), V("g1", a, 4 * C, 4)),
+            "E": lambda a: move("g", V("w0", PL * a + A, PL * a + A + C), V("g0", a, 4 * C, 4)),
+            "X": lambda q, k: [
+                lambda: affine(q, V("ab"), V("aa"), 4096.0, 4096.0 * (0.5 - A)),
+                lambda: affine(q, V("u1", 9 * t, 9 * t + 9), V("u2", 0, 9), 0.5, col(5)),
+                lambda: affine(q, V("iy"), V("ix") if t else V("ma", 16, 32), 1.0, float(A))][k](),
             "sy": lambda: scan(V("yy"), V("ff", 15, 15 + 2 * C), V("ff", 15, 15 + 2 * C), 0.0, OP.add, OP.max),
             "sh": lambda: scan(V("hd"), V("k16"), V("yy"), 0.0, OP.add, OP.min),
             "F": lambda lv: scan(V("hf", C * lv, C * lv + C), V("ff", 16 + C * lv, 16 + C * lv + C), V("kf", 0, C), 0.0, OP.max, OP.mult),
             "hf": lambda: scan(V("hf"), V("ff", 16, 16 + 2 * C), V("kf"), 0.0, OP.max, OP.mult),
+            "pa": lambda: affine("a", V("pre", 0, 16), V("hf", 15, C, 16), 1.0, 2.0 * XW),
+            "pb": lambda: tt(V("pre", 16, 32), V("hf", C + 15, 2 * C, 16), V("cn", 16, 32), OP.add),
             "pr": lambda: tt(V("pre"), V("hf", 15, 2 * C, 16), V("cn"), OP.add),
             "aa": lambda: tt(V("aa"), V("hd", 15, 2 * C, 16), V("pre"), OP.max),
             "mb": lambda: tt(V("aa", 16, 32), V("aa", 0, 16), V("aa", 16, 32), OP.min),
@@ -439,14 +474,14 @@ def rank_program(g, core, T, topo):
             "vv": lambda: tt(V("vv", 0, 9), V("u2", 0, 9), V("cv", 0, 9), OP.add),
             "ls": lambda: remote(V("il_%d" % t), V("li_%d" % (t + 1)), 3 * t + 5, "sent1"),
             "sc": lambda: cp((xw, i2), V("lanes")),
-            "ld": loads,
+            "ld": loads, "tb": table,
             "M": lambda b: tt(V("m0_0", b, 4 * C, 4), P("psx", b, C), V("h0", b, 4 * C, 4), OP.add) if t == 0 and not PLAN["acc0"] else None,
             "h4": lambda: scan(V("h4"), V("k4"), xs, 0.0, OP.add, OP.min),
-            "h6": lambda: scan(V("h16"), V("k16g"), xs, 0.0, OP.add, OP.min),
+            "h6": lambda: scan(V("h16", A * t, A * t + A), V("k16g"), xs, 0.0, OP.add, OP.min),
             "e4": lambda: ts(V("e4"), V("h4", 3, A, 4), 4.0, col(4), OP.mult, OP.add),
             "Za": lambda: move("a", V("z0", 16 * zv, 4 * A), (V("m0_%d" % t), V("e4", zv)), 0.5),
             "Zv": lambda: move("v", V("z0", 0, 16 * zv), (V("m0_%d" % t), V("e4", 0, zv)), 0.5),
-            "s1": lambda: tt(V("s1", 0, 9), V("h16", 15, A, 16), V("vv", 0, 9), OP.min),
+            "s1": lambda: tt(V("s1", 0, 9), V("h16", A * t + 15, A * t + A, 16), V("vv", 0, 9), OP.min),
             "qy": replay0,
         }
 
@@ -459,7 +494,6 @@ def rank_program(g, core, T, topo):
         play(PLAN["mid" if t < R - 1 else "end"], calls, t)
 
     TAG[0] = "z"
-    dma("a", lambda: g.scalar.dma_start(T.ol[:], T.olr[0:128:16, :]), [], [V("olr")])
     for k in range(4):
         dma("a", lambda k=k: g.scalar.dma_start(T.osc[4 * k:4 * k + 4, :], T.q2_3s[32 * k:32 * k + 4, :]), [], [V("q2_3s")])
 
@@ -523,6 +557,7 @@ def rank_program(g, core, T, topo):
             ins.then_inc(T.sem[o["sem"][0]], 16)
         elif o["kind"] == "c" and j in waited:
             ins.then_inc(T.sem[o["sem"][0]], 1)
+    g.wait_ge(T.sem.sent0, sent["sent0"])
     g.wait_ge(T.sem.sent1, sent["sent1"])
     for o in tail:
         g.wait_ge(T.sem[o["sem"][0]], 16)

from concourse.mybir import dt, AluOpType, ActivationFunctionType

C, A, R = 256, 144, 3
D = C // 2
PL = 416
XW = 528
BF, F32, F16, I32, U16, QC, QS = "bfloat16", "float32", "float16", "int32", "uint16", "float8_e4m3fn_x4", "uint8"

SCRATCH = {"psx": ("psum", [128, 2048], F32), "psy": ("psum", [128, 2048], F32)}


def _bufs(names, n, d):
    for name in names.split():
        SCRATCH[name] = ("sbuf", [128, n], d)


def _pairs(names, n):
    for name in names.split():
        _bufs(name + "c", n, QC)
        _bufs(name + "s", n, QS)


_bufs("h0 h1_0 h1_1 h1_2 h2", 4 * C, BF)
_bufs("g0", 4 * C, BF)
_bufs("hw", R * 4 * A + 4 * C, BF)
_bufs("g1 m0_0 m0_1 m0_2", 4 * C + 16, BF)
_bufs("ut vt", 512, BF)
_pairs("uraw uq vq", 128)
_pairs("wq eq", 512)
_bufs("et", 516, BF)
_pairs("q0 q1_0 qh q2_0 q2_3 l1_0 l2_0 gq0 gq1", C)
_pairs("zq0 zq1 q1_1 q1_2 l1_1 l1_2 q2_1 q2_2 l2_1 l2_2", A)
_bufs("p0s p1s mx1 thr0 ysb", C, F32)
_bufs("lanes km", C, BF)
_bufs("ff", 2 * C + 16, F16)
_bufs("yy hd hf k16 kf", 2 * C, BF)
_bufs("h4", A, F16)
_bufs("km4 k16g k4 k4a", A, BF)
_bufs("kg", C, BF)
_bufs("h16", R * A, F32)
_bufs("u1 s2", 32, F32)
_bufs("cl", 32, U16)
_bufs("pre aa ab mn ma c2 cn", 32, F32)
_bufs("ix iy", 16, F32)
_bufs("pi", 16, I32)
_bufs("list2 uoff i2", 16, U16)
_bufs("e4", A // 4, U16)
_bufs("l4", 64, U16)
_bufs("il_0 il_1 li_1 li_2", 32, U16)
_bufs("col jq jj cv u2 vv s1", 16, F32)
_bufs("xx", R * XW, BF)
_bufs("table", 2 * C + 16, F32)
_bufs("idv", 128, F32)
_bufs("w0 w1 w2", 4 * PL, BF)
_bufs("z0 z1 g1e t0", 4 * A, BF)
_bufs("olr", R * A, F32)

SEMAPHORES = ["cv", "ca", "cp", "cg", "sent0", "sent1", "sent2", "go"] + ["arr%d" % k for k in range(3 * R)] + ["d%d" % k for k in range(30)]

PLAN = {
    "h0w": 3, "acc0": 0, "z0v": 18, "g1v": 6,
    "rx0": "Q0 a3 a1 ev3 A0 S0 a0 a2 d1 ea1 ev2 ea0 q0 fa1 d2 d3 d0 fa2 fv3 s0 Q1 fa0 p0 A1 p1 c1 S1 T0 l0 T1 l1 J0 J1",
    "mid": "E0 E1 E2 E3 tb Oa0 Oa1 F1 sy F0 pb sh pa M0 aa Oa2 Oa3 u2 mb Ba0 Xa0 M2 i2 M3 Xa1 Ba1 Ba2 Ba3 sc M1 ld h4 e4 b1 Zv h6 Za ga vv qy gv b2 s1 i0 j2 rv1 ra0 rv2 ra3 z0 na0 z1 ls na1 na3 z3 na2 z2 o1 qz hv2 W1 ha1 a1 tv1 ha3 a3 ta0 ta2 tv3 a0 a2 ha0 o2 ea1 qh ea2 ev3 d2 Xa2 ev0 wa3 wv1 d0 Pv0 wv0 wa2 fa2 fv0 q0 ma d1 fa1 d3 fa3 uv0 ua2 uv1 uv5 s0 ua4 ua3 uv6 ua7 p0 p1 c1 T0 l0 T1 J0 l1 J1",
    "end": "F1 sy F0 Oa0 Oa1 Oa2 Oa3 pb pa sh u2 vq aa vv mb i2 Xa0 sc h4 e4 Zv Za h6 Xa1 b1 qy gv s1 W1 K0 j2 rv0 K1 ga ra2 rv1 z0 ra3 z1 K2 z3 z2 W2 qz ta0 tv1 K3 ta2 tv3 gv5 ga4 ga7 ga2 gv6 gv1 ga0 gv3 x1 x0 ya1 ya0",
}


def rank_program(g, core, T, topo):
    rank = T.rank_of(core)
    if rank is None:
        return
    n_ranks = len(T.cores)
    nxt, prv = T.cores[(rank + 1) % n_ranks], T.cores[(rank - 1) % n_ranks]
    rid, pid, _se = topo.addr(nxt)
    mask = topo.mask(core, nxt)
    n_out, n_in = len(topo.engines(core, nxt)), len(topo.engines(prv, core))
    Q = {"v": g.vector, "a": g.scalar, "p": g.tensor, "g": g, "s": g.sync}
    OP, AF = AluOpType, ActivationFunctionType
    ops = []
    TAG = [None]
    PLAN["ops"] = ops
    sent = {"sent0": 0, "sent1": 0, "sent2": 0}

    def V(name, a=0, b=None, s=1):
        return (name, a, SCRATCH[name][1][1] if b is None else b, s)

    def ap(v):
        if not isinstance(v, tuple):
            return v
        if len(v) == 2:
            return ap(v[0]).indirect(ap(v[1]))
        return T[v[0]][:, v[1]:v[2]] if v[3] == 1 else T[v[0]][:, v[1]:v[2]:v[3]]

    def flat(vs):
        out = []
        for v in vs:
            if isinstance(v, tuple):
                out += list(v) if len(v) == 2 else [v]
        return out

    def op(q, fn, w, r, kind="c", pre=None, sem=None):
        ops.append({"q": q, "fn": fn, "w": flat(w), "r": flat(r), "kind": kind, "pre": pre, "sem": sem, "tag": TAG[0]})

    def ts(o, i, s1, s2, o0, o1=None):
        if o1 is None:
            op("v", lambda: g.vector.tensor_scalar(ap(o), ap(i), ap(s1), None, o0), [o], [i, s1])
        else:
            op("v", lambda: g.vector.tensor_scalar(ap(o), ap(i), ap(s1), ap(s2), o0, o1), [o], [i, s1, s2])

    def tt(o, a, b, o0):
        op("v", lambda: g.vector.tensor_tensor(ap(o), ap(a), ap(b), o0), [o], [a, b])

    def cp(o, i):
        if len(o) == 2:
            op("v", lambda: g.vector.tensor_copy(ap(o), ap(i)), [o[0]], [i, o[1]])
        else:
            op("v", lambda: g.vector.tensor_copy(ap(o), ap(i)), [o], [i])

    def scan(o, a, b, init, o0, o1):
        op("v", lambda: g.vector.tensor_tensor_scan(ap(o), ap(a), ap(b), init, o0, o1), [o], [a, b])

    def fill(o, c):
        op("v", lambda: g.vector.memset(ap(o), c), [o], [])

    def act(o, i, f, scale=1.0, bias=0.0):
        kw = {k: ap(x) for k, x, plain in (("scale", scale, 1.0), ("bias", bias, 0.0)) if x != plain}
        op("a", lambda: g.scalar.activation(ap(o), ap(i), f, **kw), [o], [i, bias])

    def affine(q, o, i, scale, bias):
        if q == "a":
            act(o, i, AF.Identity, scale, bias)
        else:
            ts(o, i, scale, bias, OP.mult, OP.add)

    def move(q, o, i, scale=1.0):
        if q == "g":
            op("g", lambda: g.affine_select(ap(o), ap(i), [[0, o[2] - o[1]]], OP.is_gt, 0.0, 1, 0), [o], [i])
        elif q == "a":
            act(o, i, AF.Copy, scale)
        elif scale == 1.0:
            cp(o, i)
        else:
            ts(o, i, scale, None, OP.mult)

    def relu(q, o, i, scale):
        if q == "a":
            act(o, i, AF.Relu, scale)
        else:
            ts(o, i, 0.0, scale, OP.max, OP.mult)

    def iota(o, pat, base, cm):
        if SCRATCH[o[0]][2] == I32:
            op("g", lambda: g.iota(ap(o), pat, base, cm), [o], [])
        else:
            op("g", lambda: g.iota(ap(o), pat, base, cm, allow_small_or_imprecise_dtypes=True), [o], [])

    def quant(p, i, a=0, b=None):
        c, s = V(p + "c", a, b), V(p + "s", a, b)
        op("v", lambda: g.vector.quantize_mx(ap(c), ap(s), ap(i)), [c, s], [i])

    def mm(ps, bank, wp, wa, xp, a=0, b=None):
        wc, ws, xc, xs = V(wp + "c", wa, wa + 128), V(wp + "s", wa, wa + 128), V(xp + "c", a, b), V(xp + "s", a, b)
        o = V(ps, 512 * bank, 512 * bank + xc[2] - xc[1])
        op("p", lambda: g.tensor.matmul_mx(ap(o), ap(wc), ap(ws), ap(xc), ap(xs), True, True), [o], [wc, ws, xc, xs])

    def P(ps, bank, n):
        return V(ps, 512 * bank, 512 * bank + n)

    def dma(q, fn, w, r, pre=None):
        op(q, fn, w, r, kind="d", pre=pre)

    def remote(src, dst, k, s):
        cast = (lambda x: x.bitcast(dt.uint8)) if SCRATCH[src[0]][2] == QC else (lambda x: x)
        sent[s] += n_out
        op("g", lambda: g.remote_dma(cast(ap(dst)), cast(ap(src)), T.sem["arr%d" % k], T.sem[s], pid, rid, mask), [], [src], kind="r")

    def send(src, dst, k, s):
        remote(V(src + "c"), V(dst + "c"), k, s)
        remote(V(src + "s"), V(dst + "s"), k, s)

    def arrive(views, k, calls):
        op(None, None, views, [], kind="x", sem=("arr%d" % k, calls * n_in))

    def col(k):
        return V("col", k, k + 1)

    def G0(t, a=0, s=1):
        return V("g0", a, 4 * C, s)

    def T1(t, a=0, s=1):
        return V("hw", 4 * A * (R - 1 - t) + a, 4 * A * (R - t), s)

    def play(plan, calls, ph):
        for w in plan.split():
            TAG[0] = (ph, w if w in calls or len(w) == 2 else w[0] + "_" + w[2])
            if w in calls:
                calls[w]()
            elif len(w) == 2:
                calls[w[0]](int(w[1]))
            else:
                calls[w[0]](w[1], int(w[2]))

    h2x = V("hw", R * 4 * A)
    h0 = V("m0_0", 0, 4 * C) if PLAN["acc0"] else V("h0")
    dma("s", lambda: g.sync.dma_start(T.h1_0[:, 0:2 * C], T.x[:, 4 * C:6 * C]), [V("h1_0", 0, 2 * C)], [])
    dma("s", lambda: g.sync.dma_start(T.h1_0[:, 2 * C:4 * C], T.x[:, 6 * C:8 * C]), [V("h1_0", 2 * C, 4 * C)], [])
    dma("s", lambda: g.sync.dma_start(ap(h2x), T.x[:, 8 * C:12 * C]), [h2x], [])
    dma("s", lambda: g.sync.dma_start(T.ut[:], T.u[:]), [V("ut")], [])
    h0a, h0b = V(h0[0], 0, 2 * C), V(h0[0], 2 * C, 4 * C)
    dma("s", lambda: g.sync.dma_start(ap(h0a), T.x[:, 0:2 * C]), [h0a], [])
    if not PLAN["h0w"]:
        dma("s", lambda: g.sync.dma_start(ap(h0b), T.x[:, 2 * C:4 * C]), [h0b], [])

    def const(o, c):
        act(o, V("et", 0, o[2] - o[1]), AF.Identity, 0.0, c)

    iota(V("idv"), [[1, 128]], 0, -1)
    iota(V("pi", 0, 1), [[0, 1]], 0, 1)
    iota(V("jq"), [[16, 16]], 0, 0)
    iota(V("km"), [[0, 16], [1, 16]], 0, 0)
    iota(V("km4"), [[0, A // 4], [1, 4]], 0, 0)
    fill(V("et"), 0.0)
    fill(V("ff", 0, 16), 0.0)
    ts(V("et", 3, 515, 4), V("idv"), 0.0, None, OP.is_equal)
    ts(V("pi", 1, 2), V("pi", 0, 1), 15, None, OP.bitwise_and)
    ts(V("pi", 2, 3), V("pi", 0, 1), 2, 3, OP.arith_shift_right, OP.bitwise_and)
    ts(V("pi", 3, 4), V("pi", 0, 1), 3, None, OP.bitwise_and)
    for b in range(4):
        quant("eq", V("et", 3 - b, 515 - b), 128 * b, 128 * b + 128)
    cp(V("col", 0, 3), V("pi", 1, 4))
    cp(V("uoff", 0, 8), V("jq", 0, 8))
    for t in range(R):
        const(V("xx", XW * t, XW * t + A), float(C))
        const(V("m0_%d" % t, 4 * C, 4 * C + 16), 0.0)
    const(V("g1", 4 * C, 4 * C + 16), 0.0)
    for a in range(4):
        const(V("w1", PL * a + A + C, PL * a + PL), 0.0)
    const(V("cn", 0, 16), 2.0 * XW)
    affine("a", col(3), col(1), -2048.0, 6144.0)
    affine("a", col(5), col(0), -512.0, 7680.0)
    affine("a", col(6), col(0), -512.0, 7680.0 + A)
    affine("a", col(7), col(0), 513.0, -7680.0 - A)
    affine("a", V("jj"), V("jq"), 1.0, col(0))
    affine("a", col(4), col(3), 1.0, col(2))
    affine("a", V("cv"), V("jq"), 1.0, col(7))
    for k in range(2):
        affine("a", V("c2", 16 * k, 16 * k + 16), V("jj"), 1.0, float(A))
    affine("a", V("cn", 16, 32), V("jj"), 1.0, XW - C - 8.0)

    quant("q1_0", V("h1_0", 0, 2 * C), 0, D)
    remote(V("q1_0c", 0, D), V("l1_0c", 0, D), 0, "sent0")
    ts(V("kg"), V("km"), col(0), None, OP.is_gt)
    ts(V("k16", 0, C), V("km"), col(0), 16384.0, OP.is_equal, OP.mult)
    quant("q1_0", V("h1_0", 2 * C, 4 * C), D, C)
    remote(V("q1_0c", D, C), V("l1_0c", D, C), 0, "sent0")
    remote(V("q1_0s"), V("l1_0s"), 0, "sent0")
    ts(V("k4a"), V("km4"), col(1), 4096.0, OP.is_equal, OP.mult)
    tt(V("kf", 0, C), V("kg"), V("k16", 0, C), OP.add)
    move("a", V("k16", C, 2 * C), V("k16", 0, C))
    affine("a", V("k16g"), V("k16", 0, A), 1.0, -512.0)
    affine("a", V("k4"), V("k4a"), 1.0, -512.0)
    move("a", V("kf", 15, C, 16), V("kf", 15, C, 16), -0.25)
    move("a", V("kf", C, 2 * C), V("kf", 0, C))
    quant("q2_0", h2x)
    send("q2_0", "l2_0", 1, "sent2")
    if PLAN["h0w"] == 3:
        op("g", lambda: g.sem_inc(T.sem.go, 1), [], [])
        dma("s", lambda: g.sync.dma_start(ap(h0b), T.x[:, 2 * C:4 * C]), [h0b], [], pre=("go", 1))
    elif PLAN["h0w"]:
        dma("s", lambda: g.sync.dma_start(ap(h0b), T.x[:, 2 * C:4 * C]), [h0b], [V("q2_0s")] if PLAN["h0w"] == 2 else [],
            pre=("sent0", 3 * n_out) if PLAN["h0w"] == 1 else None)
    dma("s", lambda: g.sync.dma_start(T.wqc[:].bitcast(dt.uint8), T.wc[:]), [V("wqc")], [], pre=("sent2", 2 * n_out))
    if PLAN["acc0"]:
        dma("g", lambda: g.dma_start(T.wqs[:], T.ws[:]), [V("wqs")], [])
    else:
        dma("s", lambda: g.sync.dma_start(T.wqs[:], T.ws[:]), [V("wqs")], [])
    iota(V("lanes"), [[1, C]], 0, 0)
    quant("uraw", V("ut"))
    op("v", lambda: g.vector.tensor_copy(T.uqc[:].bitcast(dt.uint32), T.urawc[:].bitcast(dt.uint32).indirect(T.uoff[:, 0:8])),
       [V("uqc")], [V("urawc"), V("uoff", 0, 8)])
    move("a", V("uqs"), (V("uraws"), V("uoff", 0, 8)))
    mm("psy", 1, "uq", 0, "q1_0")
    move("a", V("p1s"), P("psy", 1, C))

    def logs(t):
        n = A if t else C
        at0 = ("psx", 0) if t else ("psy", 2)
        s0 = P(at0[0], at0[1], C)
        m0 = V("m0_%d" % t, 0, 4 * C)
        arrive([V("l1_%dc" % t), V("l1_%ds" % t)], 3 * t, 3 if t == 0 else 2)
        arrive([V("l2_%dc" % t), V("l2_%ds" % t)], 3 * t + 1, 2)
        if t:
            arrive([V("li_%d" % t)], 3 * t + 2, 1)

        def score1(h):
            quant("gq1", V("g1", 2 * C * h, 2 * C * h + 2 * C), D * h, D * h + D)
            mm("psy", h, "uq", 0, "gq1", D * h, D * h + D)

        def late(k):
            tt(V("ff", 16 + C + D * k, 16 + C + D * k + D), P("psy", k, D), V("mx1", D * k, D * k + D), OP.is_gt)

        def whole():
            quant("gq1", V("g1", 0, 4 * C))
            mm("psy", 0, "uq", 0, "gq1")

        def late2(lv):
            if lv:
                tt(V("ff", 16 + C, 16 + 2 * C), P("psy", 0, C), V("mx1"), OP.is_gt)
            else:
                tt(V("ff", 16, 16 + C), s0, V("thr0"), OP.is_ge)

        def own0(h):
            quant("q0", V(h0[0], 2 * C * h, 2 * C * h + 2 * C), D * h, D * h + D)
            mm("psy", 3, "uq", 0, "q0", D * h, D * h + D)

        def update(q, k):
            b, h = k % 4, k // 4
            move(q, V("g1", 2 * C * h + b, 2 * C * h + 2 * C, 4), (V("w2", PL * b, PL * b + A + C), V("li_%d" % t, 16 + 8 * h, 24 + 8 * h)))

        def update2(q, b):
            move(q, V("g1", b, 4 * C, 4), (V("w2", PL * b, PL * b + A + C), V("li_%d" % t, 16, 32)))

        def cap(q, _k):
            if q == "v":
                ts(V("kk"), V("l0"), -0.5, 2.0 ** 91, OP.add, OP.mult)
            else:
                act(V("kk"), V("l0"), AF.Identity, 2.0 ** 91, -2.0 ** 90)

        return {
            "a": lambda b: mm("psx", b, "eq", 128 * b, "l1_%d" % t),
            "e": lambda q, b: move(q, V("w0", PL * b, PL * b + A) if t else G0(t, b, 4), P("psx", b, n)),
            "w": lambda q, b: move(q, G0(t, b, 4), (V("w0", PL * b, PL * b + A + C), V("li_%d" % t, 0, 16))),
            "m": lambda b: tt(V("m0_0", b, 4 * C, 4), P("psx", b, C), V("h0", b, 4 * C, 4), OP.add),
            "ma": lambda: dma("g", lambda: g.dma_start(ap(m0), ap(G0(t)), accum_op=OP.add), [m0], [G0(t), m0]),
            "q0": lambda: quant("gq0", G0(t)),
            "s0": lambda: mm(at0[0], at0[1], "uq", 0, "gq0"),
            "d": lambda b: mm("psy", b, "eq", 128 * b, "l2_%d" % t),
            "f": lambda q, b: move(q, V("w2", PL * b, PL * b + A) if t else V("g1", b, 4 * C, 4), P("psy", b, n)),
            "u": update, "p": score1, "l": late, "pp": whole, "L": late2, "U": update2,
            "T": lambda h: tt(V("thr0", D * h, D * h + D), P("psy", h, D), V("p0s", D * h, D * h + D), OP.max),
            "TT": lambda: tt(V("thr0"), P("psy", 0, C), V("p0s"), OP.max),
            "J": lambda h: tt(V("ff", 16 + D * h, 16 + D * h + D), V(s0[0], s0[1] + D * h, s0[1] + D * h + D), V("thr0", D * h, D * h + D), OP.is_ge),
            "Q": own0, "A": lambda h: act(V("ysb", D * h, D * h + D), P("psy", 3, D), AF.Abs, 5 * 2.0 ** -26, 2.0 ** -124),
            "S": lambda h: tt(V("p0s", D * h, D * h + D), P("psy", 3, D), V("ysb", D * h, D * h + D), OP.add),
            "c1": lambda: tt(V("mx1"), s0, V("p1s"), OP.max),
            "k": cap,
            "c3": lambda: tt(V("thr0"), s0, V("kk"), OP.min),
        }

    def replay(t):
        gv = PLAN["g1v"]

        def replay1():
            quant("zq1", V("z1"))
            for a in range(4):
                mm("psy", a, "wq", 128 * a, "zq1")

        def out1():
            quant("q1_%d" % (t + 1), V("t0"))
            send("q1_%d" % (t + 1), "l1_%d" % (t + 1), 3 * t + 3, "sent1")

        def out2():
            quant("q2_%d" % (t + 1), T1(t))
            send("q2_%d" % (t + 1), "l2_%d" % (t + 1), 3 * t + 4, "sent1")

        def own1():
            quant("qh", V("h1_%d" % (t + 1)))
            mm("psy", 3, "uq", 0, "qh")

        def keys():
            tt(V("s2", 0, 9 * R), V("h16", 15, R * A, 16), V("u1", 0, 9 * R), OP.add)

        def where1():
            if t:
                tt(V("ix"), V("mn", 16, 32), V("iy"), OP.min)

        def where2():
            if t < R - 1:
                ts(V("iy"), V("ix") if t else V("ma", 16, 32), float(A), None, OP.add)
            else:
                for a in range(4):
                    ts(V("l4", 16 * a, 16 * a + 16), V("ix"), 4.0, float(a), OP.mult, OP.add)

        def once():
            quant("vq", V("vt"))

        def outputs():
            quant("q2_3", V("h2"))
            mm("psx", 0, "vq", 0, "q2_3")
            dma("s", lambda: g.sync.dma_start(T.oc[:], T.q2_3c[:].bitcast(dt.uint8)), [], [V("q2_3c")])
            move("v", V("ysb"), P("psx", 0, C))
            dma("s", lambda: g.sync.dma_start(T.y[:], T.ysb[:]), [], [V("ysb")])

        def gather_half(q, k):
            a, h = k % 4, k // 4
            move(q, V("h2", 2 * C * h + a, 2 * C * h + 2 * C, 4), (V("hw"), V("l4", 16 * a + 8 * h, 16 * a + 8 * h + 8)))

        def pack_half(h):
            quant("q2_3", V("h2", 2 * C * h, 2 * C * h + 2 * C), D * h, D * h + D)
            mm("psx", h, "vq", 0, "q2_3", D * h, D * h + D)
            dma("s", lambda: g.sync.dma_start(T.oc[:, 4 * D * h:4 * D * h + 4 * D], T.q2_3c[:, D * h:D * h + D].bitcast(dt.uint8)), [],
                [V("q2_3c", D * h, D * h + D)])

        def store_half(q, h):
            move(q, V("ysb", D * h, D * h + D), P("psx", h, D))
            dma("s", lambda: g.sync.dma_start(T.y[:, D * h:D * h + D], T.ysb[:, D * h:D * h + D]), [], [V("ysb", D * h, D * h + D)])

        return {
            "r": lambda q, a: relu(q, V("w1", PL * a, PL * a + A), P("psx", a, A), 2.0 ** -6),
            "z": lambda a: tt(V("z1", a, 4 * A, 4), (V("w1", PL * a, PL * a + PL), V("list2", 0, 9)), V("g1e", a, 4 * A, 4), OP.add),
            "n": lambda q, a: move(q, V("t0", a, 4 * A, 4), V("w1", PL * a, PL * a + A), 2.0),
            "R": lambda q, a: relu(q, V("t0", a, 4 * A, 4), P("psx", a, A), 2.0 ** -5),
            "gv": lambda: move("v", V("g1e", 0, 16 * gv), (V("g1"), V("e4", 0, gv)), 0.5) if gv else None,
            "ga": lambda: move("a", V("g1e", 16 * gv, 4 * A), (V("g1"), V("e4", gv)), 0.5),
            "j2": lambda: ts(V("list2", 0, 9), V("s1", 0, 9), col(6), None, OP.add),
            "qz": replay1,
            "h": lambda q, a: move(q, V("h1_%d" % (t + 1), a, 4 * C, 4), (V("w1", PL * a, PL * a + A + C), V("il_%d" % t, 0, 16)), 2.0),
            "t": lambda q, a: relu(q, T1(t, a, 4), P("psy", a, A), 2.0 ** -5),
            "o1": out1, "o2": out2, "qh": own1,
            "P": lambda q, _k: move(q, V("p1s"), P("psy", 3, C)),
            "K0": keys, "K1": lambda: cp(V("cl", 0, 9 * R), V("s2", 0, 9 * R)),
            "K2": lambda: move("a", V("olr"), (V("table"), V("cl", 0, 9 * R))),
            "K3": lambda: dma("s", lambda: g.sync.dma_start(T.ol[:], T.olr[0:128:16, :]), [], [V("olr")]),
            "W1": where1, "W2": where2, "vq": once,
            "G": lambda q, a: move(q, V("h2", a, 4 * C, 4), (V("hw"), V("l4", 16 * a, 16 * a + 16))),
            "xx": outputs, "g": gather_half, "x": pack_half, "y": store_half,
        }

    def lists(t):
        i2, xw, xs = V("i2"), V("xx", XW * t, XW * t + XW), V("xx", XW * t, XW * t + A)
        zv = PLAN["z0v"]

        def loads():
            dma("s", lambda: g.sync.dma_start(T["m0_%d" % (t + 1)][:, 0:4 * C], T.x[:, 0:4 * C]), [V("m0_%d" % (t + 1), 0, 4 * C)],
                [V("m0_%d" % t, 0, 4 * C)])
            if t == 0:
                dma("g", lambda: g.dma_start(T.vt[:], T.v[:]), [V("vt")], [])

        def table():
            if t == 0:
                iota(V("table", 0, 2 * C), [[1, 2 * C]], 0, 0)
                iota(V("table", 2 * C, 2 * C + 16), [[0, 16]], -1, 0)

        def replay0():
            quant("zq0", V("z0"))
            for a in range(4):
                mm("psx", a, "wq", 128 * a, "zq0")

        return {
            "O": lambda q, a: move(q, V("w1", PL * a + A, PL * a + A + C), V("h1_%d" % t, a, 4 * C, 4), 0.5),
            "B": lambda q, a: move(q, V("w2", PL * a + A, PL * a + A + C), V("g1", a, 4 * C, 4)),
            "C": lambda q, a: move(q, V("w0", PL * a + A, PL * a + A + C), V("g0", a, 4 * C, 4)),
            "D": lambda a: move("g", V("w2", PL * a + A, PL * a + A + C), V("g1", a, 4 * C, 4)),
            "E": lambda a: move("g", V("w0", PL * a + A, PL * a + A + C), V("g0", a, 4 * C, 4)),
            "X": lambda q, k: [
                lambda: affine(q, V("ab"), V("aa"), 4096.0, 4096.0 * (0.5 - A)),
                lambda: affine(q, V("u1", 9 * t, 9 * t + 9), V("u2", 0, 9), 0.5, col(5)),
                lambda: affine(q, V("iy"), V("ix") if t else V("ma", 16, 32), 1.0, float(A))][k](),
            "sy": lambda: scan(V("yy"), V("ff", 15, 15 + 2 * C), V("ff", 15, 15 + 2 * C), 0.0, OP.add, OP.max),
            "sh": lambda: scan(V("hd"), V("k16"), V("yy"), 0.0, OP.add, OP.min),
            "F": lambda lv: scan(V("hf", C * lv, C * lv + C), V("ff", 16 + C * lv, 16 + C * lv + C), V("kf", 0, C), 0.0, OP.max, OP.mult),
            "hf": lambda: scan(V("hf"), V("ff", 16, 16 + 2 * C), V("kf"), 0.0, OP.max, OP.mult),
            "pa": lambda: affine("a", V("pre", 0, 16), V("hf", 15, C, 16), 1.0, 2.0 * XW),
            "pb": lambda: tt(V("pre", 16, 32), V("hf", C + 15, 2 * C, 16), V("cn", 16, 32), OP.add),
            "pr": lambda: tt(V("pre"), V("hf", 15, 2 * C, 16), V("cn"), OP.add),
            "aa": lambda: tt(V("aa"), V("hd", 15, 2 * C, 16), V("pre"), OP.max),
            "mb": lambda: tt(V("aa", 16, 32), V("aa", 0, 16), V("aa", 16, 32), OP.min),
            "i2": lambda: ts(i2, V("aa", 16, 32), 0.25, None, OP.add),
            "b0": lambda: ts(V("ab"), V("aa"), 0.5 - A, 4096.0, OP.add, OP.mult),
            "b1": lambda: tt(V("mn"), V("aa"), V("ab"), OP.max),
            "b2": lambda: tt(V("ma"), V("mn"), V("c2"), OP.min),
            "i0": lambda: cp(V("il_%d" % t), V("ma")),
            "u2": lambda: ts(V("u2", 0, 9), V("jj", 0, 9), V("yy", C, C + 1), 512.0, OP.is_ge, OP.mult),
            "vv": lambda: tt(V("vv", 0, 9), V("u2", 0, 9), V("cv", 0, 9), OP.add),
            "ls": lambda: remote(V("il_%d" % t), V("li_%d" % (t + 1)), 3 * t + 5, "sent1"),
            "sc": lambda: cp((xw, i2), V("lanes")),
            "ld": loads, "tb": table,
            "M": lambda b: tt(V("m0_0", b, 4 * C, 4), P("psx", b, C), V("h0", b, 4 * C, 4), OP.add) if t == 0 and not PLAN["acc0"] else None,
            "h4": lambda: scan(V("h4"), V("k4"), xs, 0.0, OP.add, OP.min),
            "h6": lambda: scan(V("h16", A * t, A * t + A), V("k16g"), xs, 0.0, OP.add, OP.min),
            "e4": lambda: ts(V("e4"), V("h4", 3, A, 4), 4.0, col(4), OP.mult, OP.add),
            "Za": lambda: move("a", V("z0", 16 * zv, 4 * A), (V("m0_%d" % t), V("e4", zv)), 0.5),
            "Zv": lambda: move("v", V("z0", 0, 16 * zv), (V("m0_%d" % t), V("e4", 0, zv)), 0.5),
            "s1": lambda: tt(V("s1", 0, 9), V("h16", A * t + 15, A * t + A, 16), V("vv", 0, 9), OP.min),
            "qy": replay0,
        }

    play(PLAN["rx0"], logs(0), "s")
    for t in range(R):
        calls = lists(t)
        calls.update(replay(t))
        if t < R - 1:
            calls.update(logs(t + 1))
        play(PLAN["mid" if t < R - 1 else "end"], calls, t)

    TAG[0] = "z"
    for k in range(4):
        dma("a", lambda k=k: g.scalar.dma_start(T.osc[4 * k:4 * k + 4, :], T.q2_3s[32 * k:32 * k + 4, :]), [], [V("q2_3s")])

    def bits(v):
        n = (v[2] - v[1] + v[3] - 1) // v[3]
        return ((1 << (n * v[3])) - 1) // ((1 << v[3]) - 1) << v[1]

    def banks(v):
        return ((1 << ((v[2] - 1) // 512 + 1)) - 1) >> (v[1] // 512) << (v[1] // 512)

    touch = {}
    known = {q: 0 for q in Q}
    ran = {q: 0 for q in Q}
    waited = set()
    for j, o in enumerate(ops):
        deps = set()
        for wr, vs in ((True, o["w"]), (False, o["r"])):
            for v in vs:
                m, bk = bits(v), banks(v) if SCRATCH[v[0]][0] == "psum" else 0
                for (i, mi, bi, wi) in touch.get(v[0], []):
                    if i != j and (((wr or wi) and mi & m) or (bi & bk and ops[i]["q"] != o["q"])):
                        deps.add(i)
                touch.setdefault(v[0], []).append((j, m, bk, wr))
        q = o["q"]
        o["waits"] = []
        if q is None:
            o["done"] = 1 << j
            continue
        for i in sorted(deps, reverse=True):
            if not known[q] >> i & 1:
                o["waits"].append(i)
                waited.add(i)
                known[q] |= ops[i]["done"]
        if o["kind"] == "c":
            ran[q] |= 1 << j
            o["done"] = known[q] | ran[q]
        else:
            o["done"] = known[q] | 1 << j
    count = {q: 0 for q in Q}
    n_d = 0
    tail = []
    for j, o in enumerate(ops):
        if o["kind"] == "c" and j in waited:
            count[o["q"]] += 1
            o["sem"] = ("c" + o["q"], count[o["q"]])
        elif o["kind"] == "d":
            o["sem"] = ("d%d" % n_d, 16)
            n_d += 1
            if j not in waited:
                tail.append(o)
    for j, o in enumerate(ops):
        if o["q"] is None:
            continue
        e = Q[o["q"]]
        if o["pre"] is not None:
            e.wait_ge(T.sem[o["pre"][0]], o["pre"][1])
        for i in o["waits"]:
            e.wait_ge(T.sem[ops[i]["sem"][0]], ops[i]["sem"][1])
        ins = o["fn"]()
        if o["kind"] == "d":
            ins.then_inc(T.sem[o["sem"][0]], 16)
        elif o["kind"] == "c" and j in waited:
            ins.then_inc(T.sem[o["sem"][0]], 1)
    g.wait_ge(T.sem.sent0, sent["sent0"])
    g.wait_ge(T.sem.sent1, sent["sent1"])
    for o in tail:
        g.wait_ge(T.sem[o["sem"][0]], 16)
